import numpy as np
import ml_dtypes


def mxq(x, axis, fmt="e4m3"):
    dtype, down = {"e4m3": (ml_dtypes.float8_e4m3fn, 7), "e5m2": (ml_dtypes.float8_e5m2, 14)}[fmt]
    v = np.moveaxis(np.asarray(x, np.float32).astype(ml_dtypes.bfloat16).astype(np.float64), axis, -1)
    blocks = v.reshape(v.shape[:-1] + (-1, 32))
    amax = np.abs(blocks).max(-1, keepdims=True)
    byte = np.maximum(np.where(amax > 0, np.frexp(amax)[1] - 1 + 127, 0) - down, 1)
    scale = np.exp2(byte - 127.0)
    codes = (blocks / scale).astype(np.float32).astype(dtype).astype(np.float64)
    return np.moveaxis((codes * scale).reshape(v.shape), -1, axis)


WIDE = False


def mx_kscale(k):
    if not WIDE:
        return np.ones(k)
    levels = np.array([24, -24, 12, -12, 0])
    if k % 512:
        return np.exp2(np.random.permutation(np.resize(levels, k // 32))).repeat(32)
    a = np.empty((k // 512, 16))
    for p in range(k // 512):
        a[p, :8] = np.random.permutation(np.resize(levels, 8))
        for g in range(8):
            far = levels[np.abs(levels - a[p, g]) >= 10]
            a[p, g + 8] = far[np.random.randint(len(far))]
    return np.exp2(a.ravel()).repeat(32)


def f64(x):
    return np.asarray(x).astype(np.float64)


def striped(idx):
    return np.tile(idx.reshape(-1, 16).T, (8, 1)).astype(np.uint16)


def unstriped(offs):
    return offs[:16].T.reshape(-1).astype(np.int64)


E2M1 = np.array([0.0, 0.5, 1.0, 1.5, 2.0, 3.0, 4.0, 6.0, -0.0, -0.5, -1.0, -1.5, -2.0, -3.0, -4.0, -6.0])


def pack_weight(w, fmt):
    k, n = w.shape
    w = f64(np.asarray(w, np.float32).astype(ml_dtypes.bfloat16)).reshape(k // 32, 32, n)
    amax = np.abs(w).max(1)
    if fmt == "e4m3":
        byte = np.frexp(amax)[1] - 1 + 127 - 7
    else:
        mant, ex = np.frexp(amax / 6.0)
        byte = np.where(mant > 0.5, ex, ex - 1) + 127
    byte = np.clip(np.where(amax > 0, byte, 1), 1, 254)
    scaled = (w * np.exp2(127.0 - byte)[:, None, :]).reshape(k, n).astype(np.float32)
    by_word = np.ascontiguousarray(scaled.reshape(k // 512, 128, 4, n).transpose(0, 1, 3, 2))
    if fmt == "e4m3":
        words = by_word.astype(ml_dtypes.float8_e4m3fn).view(np.uint8)
    else:
        c = by_word.astype(ml_dtypes.float4_e2m1fn).view(np.uint8) & 0xF
        words = (c[..., 0::2] | (c[..., 1::2] << 4)).reshape(k // 512, 128, 2 * n)
    return np.ascontiguousarray(words), np.ascontiguousarray(byte.astype(np.uint8).reshape(k // 512, 16, n))


def unpack_weight(words, scales, fmt):
    g, _, n = scales.shape
    words = np.ascontiguousarray(words).reshape(g, 128, n, -1)
    if fmt == "e4m3":
        vals = words.view(ml_dtypes.float8_e4m3fn).astype(np.float64)
    else:
        nib = np.empty((g, 128, n, 4), np.uint8)
        nib[..., 0::2] = words & 0xF
        nib[..., 1::2] = words >> 4
        vals = E2M1[nib]
    vals = vals * np.repeat(np.exp2(scales.astype(np.float64) - 127.0), 8, axis=1)[..., None]
    return vals.transpose(0, 1, 3, 2).reshape(g * 512, n)


def pack_table4(v):
    words, scales = pack_weight(v, "e2m1")
    g, t = words.shape[0] // 2, v.shape[1]
    return np.ascontiguousarray(words.reshape(g, 2, 128, t, 2).transpose(0, 2, 3, 1, 4).reshape(g, 128, t, 4)), scales


def unpack_table4(words, scales):
    g, _, t, _ = words.shape
    return unpack_weight(words.reshape(g, 128, t, 2, 2).transpose(0, 3, 1, 2, 4).reshape(2 * g, 128, 2 * t), scales, "e2m1")


def split(x):
    m, e = np.frexp(f64(x))
    hi = np.ldexp(np.trunc(16.0 * m) / 16.0, e)
    return hi, f64(x) - hi


def sigm(f):
    return 1.0 / (1.0 + np.exp(-np.maximum(f, -700.0)))


K, N, T, J = 1024, 256, 2048, 1024


def setup_inputs():
    n = np.random.standard_normal
    s = mx_kscale(K)[:, None]
    p_tab = pack_table4(n((K, T)) * s)
    p_wg = pack_weight(n((K, N)) / np.sqrt(K) / s, "e2m1")
    return {
        "tab_words": p_tab[0],
        "tab_scales": p_tab[1],
        "wg_words": p_wg[0],
        "wg_scales": p_wg[1],
        "wh": (n((K, N)) / np.sqrt(K) / s).astype(np.float32),
        "bg": (0.3 * n(N) - 1.0).astype(np.float32),
        "rT": (n((N, T))).astype(np.float32),
        "offs": striped(np.random.permutation(T)[:J]),
    }


def reference(tab_words, tab_scales, wg_words, wg_scales, wh, bg, rT, offs):
    idx = unstriped(offs)
    tab_ = unpack_table4(tab_words, tab_scales)[:, idx]
    wg_ = unpack_weight(wg_words, wg_scales, "e2m1")
    wh_hi, wh_lo = split(wh)
    wh_hi_, wh_lo_ = mxq(wh_hi, 0, "e4m3"), mxq(wh_lo, 0, "e4m3")
    ga = wg_.T @ tab_
    gate = sigm(ga + f64(bg)[:, None])
    ha = wh_hi_.T @ tab_ + wh_lo_.T @ tab_
    return f64(rT)[:, idx] + gate * (np.maximum(ha, 0.0) - f64(rT)[:, idx])

@@ -1,0 +1,174 @@
+from contextlib import ExitStack
+
+import concourse.mybir as mybir
+
+K, N, T, J = 1024, 256, 2048, 1024
+FLOPS = 3 * 2 * K * N * J
+
+F32 = mybir.dt.float32
+BF16 = mybir.dt.bfloat16
+I32 = mybir.dt.int32
+U32 = mybir.dt.uint32
+U16 = mybir.dt.uint16
+U8 = mybir.dt.uint8
+FP8X4 = mybir.dt.float8_e4m3fn_x4
+FP4X4 = mybir.dt.float4_e2m1fn_x4
+ALU = mybir.AluOpType
+ACT = mybir.ActivationFunctionType
+
+P = 128
+PACK = 4
+PASSES = K // (P * PACK)
+N_TILES = N // P
+J_TILE = 512
+J_TILES = J // J_TILE
+QUADS = 4
+HI_MASK = -983056
+SHIFT_ROWS = 112
+
+
+def tile_list_hwayt_hl_relu_kernel(
+    tc, tab_words, tab_scales, wg_words, wg_scales, wh, bg, rT, offs, out
+):
+    nc = tc.nc
+    with ExitStack() as ctx:
+        keep = ctx.enter_context(tc.tile_pool(name="keep", bufs=1))
+        psum = ctx.enter_context(tc.psum_pool(name="psum", bufs=1))
+
+        offsets = keep.tile([P, J // 16], U16, name="offsets")
+        nc.sync.dma_start(offsets[:], offs)
+
+        scale_rows = keep.tile([P, T], U8, name="scale_rows", align_bytes=64)
+        nc.vector.memset(scale_rows[:].bitcast(I32), 0)
+        for q in range(QUADS):
+            nc.scalar.dma_start(
+                out=scale_rows[32 * q : 32 * q + 8, :].bitcast(I32),
+                in_=tab_scales[:, 4 * q : 4 * q + 4, :].bitcast(I32),
+            )
+
+        words = keep.tile([P, T], U32, name="words", align_bytes=64)
+        nc.sync.dma_start(
+            out=words[:].bitcast(I32), in_=tab_words[0].rearrange("p t b -> p (t b)").bitcast(I32)
+        )
+
+        wh_raw = []
+        for a in range(PASSES):
+            raw = keep.tile([P, PACK, N], F32, name="wh_raw%d" % a, align_bytes=64)
+            nc.sync.dma_start(
+                out=raw[:], in_=wh[a * P * PACK : (a + 1) * P * PACK, :].rearrange("(p i) n -> p i n", i=PACK)
+            )
+            wh_raw.append(raw)
+
+        wg_codes = keep.tile([P, PASSES, 2 * N], U8, name="wg_codes", align_bytes=64)
+        nc.sync.dma_start(out=wg_codes[:].bitcast(I32), in_=wg_words.rearrange("a p b -> p a b").bitcast(I32))
+
+        bias = keep.tile([P, N_TILES], F32, name="bias")
+        with nc.allow_non_contiguous_dma(reason="one bias value for each partition"):
+            nc.sync.dma_start(out=bias[:], in_=bg.rearrange("(c p) -> p c", p=P))
+
+        carried = []
+        for c in range(N_TILES):
+            rows = keep.tile([P, T], F32, name="carried%d" % c, align_bytes=64)
+            nc.sync.dma_start(out=rows[:], in_=rT[c * P : (c + 1) * P, :])
+            carried.append(rows)
+
+        wg_planes = keep.tile([P, PASSES, N], U8, name="wg_planes", align_bytes=64)
+        nc.gpsimd.memset(wg_planes[:].bitcast(I32), 0)
+        for q in range(QUADS):
+            nc.gpsimd.dma_start(
+                out=wg_planes[32 * q : 32 * q + 4, :, :].bitcast(I32),
+                in_=wg_scales[:, 4 * q : 4 * q + 4, :].rearrange("a r n -> r a n").bitcast(I32),
+            )
+
+        warm = keep.tile([P, N_TILES], F32, name="warm")
+        seed = keep.tile([P, N_TILES], F32, name="seed")
+        nc.gpsimd.memset(seed[:], 0.0)
+        nc.scalar.activation(warm[:], seed[:], ACT.Sigmoid)
+
+        picked_scales = keep.tile([P, J], U8, name="picked_scales", align_bytes=64)
+        plane1 = keep.tile([P, J], U8, name="plane1", align_bytes=64)
+        nc.vector.memset(plane1[:].bitcast(I32), 0)
+        nc.vector.tensor_copy(picked_scales[:], scale_rows[:].indirect(offsets[:]))
+        nc.scalar.dma_start(
+            out=plane1[0:SHIFT_ROWS, :].bitcast(I32), in_=picked_scales[4 : 4 + SHIFT_ROWS, :].bitcast(I32)
+        )
+        tab_planes = [picked_scales, plane1]
+
+        picked_words = keep.tile([P, J], U32, name="picked_words", align_bytes=64)
+        nc.vector.tensor_copy(picked_words[:], words[:].indirect(offsets[:]))
+        tab_codes = keep.tile([P, PASSES, 2 * J], U8, name="tab_codes", align_bytes=64)
+        nc.vector.tensor_copy(
+            tab_codes[:].bitcast(U16), picked_words[:].bitcast(U16).rearrange("p (j d) -> p d j", d=PASSES)
+        )
+
+        def tab_operand(a, jt):
+            codes = tab_codes[:, a, 2 * jt * J_TILE : 2 * (jt + 1) * J_TILE].bitcast(FP4X4)
+            return codes, tab_planes[a][:, jt * J_TILE : (jt + 1) * J_TILE]
+
+        wh_codes, wh_planes = [], []
+        for a in range(PASSES):
+            woven = keep.tile([P, N, PACK], F32, name="woven%d" % a, align_bytes=64)
+            nc.scalar.copy(out=woven[:], in_=wh_raw[a][:].rearrange("p i n -> p n i"))
+            flat = woven[:].rearrange("p n i -> p (n i)")
+            upper = keep.tile([P, N * PACK], BF16, name="upper%d" % a, align_bytes=64)
+            nc.scalar.copy(out=upper[:], in_=flat.bitcast(BF16)[:, 1 : 2 * N * PACK : 2])
+            parts = keep.tile([P, 2, N * PACK], BF16, name="parts%d" % a, align_bytes=64)
+            nc.vector.tensor_scalar(
+                parts[:, 0, :].bitcast(I32), upper[:].bitcast(I32), HI_MASK, None, ALU.bitwise_and
+            )
+            nc.vector.tensor_tensor(parts[:, 1, :], flat, parts[:, 0, :], ALU.subtract)
+            codes = keep.tile([P, 2 * N], U32, name="wh_codes%d" % a, align_bytes=64)
+            planes = keep.tile([P, 2 * N], U8, name="wh_planes%d" % a, align_bytes=64)
+            nc.vector.quantize_mx(
+                out=codes[:].bitcast(FP8X4), scales=planes[:], in_=parts[:].rearrange("p h x -> p (h x)")
+            )
+            wh_codes.append(codes)
+            wh_planes.append(planes)
+
+        gates, kept = [], []
+        for c in range(N_TILES):
+            gate = keep.tile([P, J], F32, name="gate%d" % c, align_bytes=64)
+            rest = keep.tile([P, J], F32, name="rest%d" % c, align_bytes=64)
+            for jt in range(J_TILES):
+                cols = slice(jt * J_TILE, (jt + 1) * J_TILE)
+                acc = psum.tile([P, J_TILE], F32, name="ga%d%d" % (c, jt))
+                for a in range(PASSES):
+                    codes, plane = tab_operand(a, jt)
+                    nc.tensor.matmul_mx(
+                        out=acc[:],
+                        lhsT=wg_codes[:, a, 2 * c * P : 2 * (c + 1) * P].bitcast(FP4X4),
+                        lhsT_scale=wg_planes[:, a, c * P : (c + 1) * P],
+                        rhs=codes,
+                        rhs_scale=plane,
+                        start=(a == 0),
+                        stop=(a == PASSES - 1),
+                    )
+                nc.scalar.activation(gate[:, cols], acc[:], ACT.Sigmoid, bias=bias[:, c : c + 1])
+                nc.scalar.activation(rest[:, cols], gate[:, cols], ACT.Copy, bias=1.0, scale=-1.0)
+            gates.append(gate)
+            kept.append(rest)
+
+        for c in range(N_TILES):
+            stay = keep.tile([P, J], F32, name="stay%d" % c, align_bytes=64)
+            nc.vector.tensor_tensor(stay[:], carried[c][:].indirect(offsets[:]), kept[c][:], ALU.mult)
+            for jt in range(J_TILES):
+                cols = slice(jt * J_TILE, (jt + 1) * J_TILE)
+                acc = psum.tile([P, J_TILE], F32, name="ha%d%d" % (c, jt))
+                steps = [(a, h) for a in range(PASSES) for h in range(2)]
+                for s, (a, h) in enumerate(steps):
+                    codes, plane = tab_operand(a, jt)
+                    wcols = slice(h * N + c * P, h * N + (c + 1) * P)
+                    nc.tensor.matmul_mx(
+                        out=acc[:],
+                        lhsT=wh_codes[a][:, wcols].bitcast(FP8X4),
+                        lhsT_scale=wh_planes[a][:, wcols],
+                        rhs=codes,
+                        rhs_scale=plane,
+                        start=(s == 0),
+                        stop=(s == len(steps) - 1),
+                    )
+                made = keep.tile([P, J_TILE], F32, name="made%d%d" % (c, jt), align_bytes=64)
+                nc.vector.scalar_tensor_tensor(made[:], acc[:], 0.0, gates[c][:, cols], ALU.max, ALU.mult)
+                result = keep.tile([P, J_TILE], F32, name="result%d%d" % (c, jt), align_bytes=64)
+                nc.vector.tensor_tensor(result[:], made[:], stay[:, cols], ALU.add)
+                nc.sync.dma_start(out=out[c * P : (c + 1) * P, cols], in_=result[:])

@@ -23,8 +23,12 @@ N_TILES = N // P
 J_TILE = 512
 J_TILES = J // J_TILE
 QUADS = 4
-HI_MASK = -983056
-SHIFT_ROWS = 112
+QUAD = 32
+HI_MASK = 0xFFF0FFF0 - (1 << 32)
+LIVE = 24
+SPAN = 100
+KB = 1024
+Y = 8 * KB
 
 
 def tile_list_hwayt_hl_relu_kernel(
@@ -33,91 +37,97 @@ def tile_list_hwayt_hl_relu_kernel(
     nc = tc.nc
     with ExitStack() as ctx:
         keep = ctx.enter_context(tc.tile_pool(name="keep", bufs=1))
+        reuse = ctx.enter_context(tc.tile_pool(name="reuse", bufs=1))
         psum = ctx.enter_context(tc.psum_pool(name="psum", bufs=1))
 
         offsets = keep.tile([P, J // 16], U16, name="offsets")
         nc.sync.dma_start(offsets[:], offs)
 
-        scale_rows = keep.tile([P, T], U8, name="scale_rows", align_bytes=64)
-        nc.vector.memset(scale_rows[:].bitcast(I32), 0)
+        scale_rows = reuse.tile([P, T], U8, name="scale_rows", align_bytes=64, offset=0)
         for q in range(QUADS):
-            nc.scalar.dma_start(
-                out=scale_rows[32 * q : 32 * q + 8, :].bitcast(I32),
+            nc.sync.dma_start(
+                out=scale_rows[QUAD * q + LIVE : QUAD * (q + 1), :].bitcast(I32),
                 in_=tab_scales[:, 4 * q : 4 * q + 4, :].bitcast(I32),
             )
+        for q in range(QUADS):
+            nc.vector.memset(scale_rows[QUAD * q : QUAD * q + LIVE, :].bitcast(I32), 0)
 
+        def load_wh(a, raw):
+            rows = wh[a * P * PACK : (a + 1) * P * PACK, :]
+            nc.sync.dma_start(out=raw[:], in_=rows.rearrange("(p i) n -> p i n", i=PACK))
+
+        wh_raw = [
+            keep.tile([P, PACK, N], F32, name="wh_raw0", align_bytes=64),
+            keep.tile([P, PACK, N], F32, name="wh_raw1", align_bytes=64),
+        ]
+        load_wh(0, wh_raw[0])
         words = keep.tile([P, T], U32, name="words", align_bytes=64)
         nc.sync.dma_start(
             out=words[:].bitcast(I32), in_=tab_words[0].rearrange("p t b -> p (t b)").bitcast(I32)
         )
-
-        wh_raw = []
-        for a in range(PASSES):
-            raw = keep.tile([P, PACK, N], F32, name="wh_raw%d" % a, align_bytes=64)
-            nc.sync.dma_start(
-                out=raw[:], in_=wh[a * P * PACK : (a + 1) * P * PACK, :].rearrange("(p i) n -> p i n", i=PACK)
-            )
-            wh_raw.append(raw)
-
-        wg_codes = keep.tile([P, PASSES, 2 * N], U8, name="wg_codes", align_bytes=64)
-        nc.sync.dma_start(out=wg_codes[:].bitcast(I32), in_=wg_words.rearrange("a p b -> p a b").bitcast(I32))
+        load_wh(1, wh_raw[1])
 
         bias = keep.tile([P, N_TILES], F32, name="bias")
         with nc.allow_non_contiguous_dma(reason="one bias value for each partition"):
             nc.sync.dma_start(out=bias[:], in_=bg.rearrange("(c p) -> p c", p=P))
 
-        carried = []
-        for c in range(N_TILES):
-            rows = keep.tile([P, T], F32, name="carried%d" % c, align_bytes=64)
-            nc.sync.dma_start(out=rows[:], in_=rT[c * P : (c + 1) * P, :])
-            carried.append(rows)
+        wg_codes = keep.tile([P, PASSES, 2 * N], U8, name="wg_codes", align_bytes=64)
+        nc.sync.dma_start(out=wg_codes[:].bitcast(I32), in_=wg_words.rearrange("a p b -> p a b").bitcast(I32))
 
         wg_planes = keep.tile([P, PASSES, N], U8, name="wg_planes", align_bytes=64)
         nc.gpsimd.memset(wg_planes[:].bitcast(I32), 0)
         for q in range(QUADS):
-            nc.gpsimd.dma_start(
-                out=wg_planes[32 * q : 32 * q + 4, :, :].bitcast(I32),
+            nc.sync.dma_start(
+                out=wg_planes[QUAD * q : QUAD * q + 4, :, :].bitcast(I32),
                 in_=wg_scales[:, 4 * q : 4 * q + 4, :].rearrange("a r n -> r a n").bitcast(I32),
             )
+        carried0 = keep.tile([P, T], F32, name="carried0", align_bytes=64, tag="codes1")
+        nc.sync.dma_start(out=carried0[:], in_=rT[0:P, :])
+
+        tab_planes = keep.tile([P, PASSES, J], U8, name="tab_planes", align_bytes=64)
+        nc.vector.memset(tab_planes[P - QUAD : P, :, :].bitcast(I32), 0)
 
         warm = keep.tile([P, N_TILES], F32, name="warm")
         seed = keep.tile([P, N_TILES], F32, name="seed")
         nc.gpsimd.memset(seed[:], 0.0)
         nc.scalar.activation(warm[:], seed[:], ACT.Sigmoid)
+        minus_bias = keep.tile([P, N_TILES], F32, name="minus_bias")
+        nc.scalar.activation(minus_bias[:], bias[:], ACT.Copy, scale=-1.0)
 
         picked_scales = keep.tile([P, J], U8, name="picked_scales", align_bytes=64)
-        plane1 = keep.tile([P, J], U8, name="plane1", align_bytes=64)
-        nc.vector.memset(plane1[:].bitcast(I32), 0)
         nc.vector.tensor_copy(picked_scales[:], scale_rows[:].indirect(offsets[:]))
-        nc.scalar.dma_start(
-            out=plane1[0:SHIFT_ROWS, :].bitcast(I32), in_=picked_scales[4 : 4 + SHIFT_ROWS, :].bitcast(I32)
-        )
-        tab_planes = [picked_scales, plane1]
-
-        picked_words = keep.tile([P, J], U32, name="picked_words", align_bytes=64)
-        nc.vector.tensor_copy(picked_words[:], words[:].indirect(offsets[:]))
-        tab_codes = keep.tile([P, PASSES, 2 * J], U8, name="tab_codes", align_bytes=64)
-        nc.vector.tensor_copy(
-            tab_codes[:].bitcast(U16), picked_words[:].bitcast(U16).rearrange("p (j d) -> p d j", d=PASSES)
-        )
-
-        def tab_operand(a, jt):
-            codes = tab_codes[:, a, 2 * jt * J_TILE : 2 * (jt + 1) * J_TILE].bitcast(FP4X4)
-            return codes, tab_planes[a][:, jt * J_TILE : (jt + 1) * J_TILE]
-
-        wh_codes, wh_planes = [], []
         for a in range(PASSES):
+            first = LIVE + 4 * a
+            nc.sync.dma_start(
+                out=tab_planes[0:SPAN, a, :].bitcast(I32), in_=picked_scales[first : first + SPAN, :].bitcast(I32)
+            )
+
+        carried1 = reuse.tile([P, T], F32, name="carried1", align_bytes=64, offset=0)
+        nc.sync.dma_start(out=carried1[:], in_=rT[P : 2 * P, :])
+
+        def split(a):
+            upper = keep.tile([P, N, PACK], BF16, name="upper%d" % a, align_bytes=64, tag="upper%d" % a)
+            halves = wh_raw[a][:].bitcast(BF16).rearrange("p i (n e) -> p n i e", e=2)
+            nc.scalar.copy(out=upper[:], in_=halves[:, :, :, 1])
             woven = keep.tile([P, N, PACK], F32, name="woven%d" % a, align_bytes=64)
             nc.scalar.copy(out=woven[:], in_=wh_raw[a][:].rearrange("p i n -> p n i"))
-            flat = woven[:].rearrange("p n i -> p (n i)")
-            upper = keep.tile([P, N * PACK], BF16, name="upper%d" % a, align_bytes=64)
-            nc.scalar.copy(out=upper[:], in_=flat.bitcast(BF16)[:, 1 : 2 * N * PACK : 2])
-            parts = keep.tile([P, 2, N * PACK], BF16, name="parts%d" % a, align_bytes=64)
+            parts = reuse.tile([P, 2, N * PACK], BF16, name="parts%d" % a, align_bytes=64, offset=Y + 2 * KB)
             nc.vector.tensor_scalar(
-                parts[:, 0, :].bitcast(I32), upper[:].bitcast(I32), HI_MASK, None, ALU.bitwise_and
+                parts[:, 0, :].bitcast(I32),
+                upper[:].rearrange("p n i -> p (n i)").bitcast(I32),
+                HI_MASK,
+                None,
+                ALU.bitwise_and,
             )
-            nc.vector.tensor_tensor(parts[:, 1, :], flat, parts[:, 0, :], ALU.subtract)
-            codes = keep.tile([P, 2 * N], U32, name="wh_codes%d" % a, align_bytes=64)
+            nc.gpsimd.tensor_tensor(
+                parts[:, 1, :], woven[:].rearrange("p n i -> p (n i)"), parts[:, 0, :], ALU.subtract
+            )
+            return parts
+
+        wh_codes, wh_planes = [], []
+
+        def quantise(a, parts):
+            codes = keep.tile([P, 2 * N], U32, name="wh_codes%d" % a, align_bytes=64, tag="codes%d" % a)
             planes = keep.tile([P, 2 * N], U8, name="wh_planes%d" % a, align_bytes=64)
             nc.vector.quantize_mx(
                 out=codes[:].bitcast(FP8X4), scales=planes[:], in_=parts[:].rearrange("p h x -> p (h x)")
@@ -125,10 +135,31 @@ def tile_list_hwayt_hl_relu_kernel(
             wh_codes.append(codes)
             wh_planes.append(planes)
 
-        gates, kept = [], []
+        parts0 = split(0)
+
+        picked_words = keep.tile([P, J], U32, name="picked_words", align_bytes=64, tag="upper0")
+        nc.vector.tensor_copy(picked_words[:], words[:].indirect(offsets[:]))
+        tab_codes = keep.tile([P, PASSES, 2 * J], U8, name="tab_codes", align_bytes=64)
+        nc.vector.tensor_copy(
+            tab_codes[:].bitcast(U16), picked_words[:].bitcast(U16).rearrange("p (j d) -> p d j", d=PASSES)
+        )
+        quantise(0, parts0)
+
+        parts1 = split(1)
+        picked0 = keep.tile([P, J], F32, name="picked0", align_bytes=64, tag="upper1")
+        nc.vector.tensor_copy(picked0[:], carried0[:].indirect(offsets[:]))
+        quantise(1, parts1)
+        picked1 = reuse.tile([P, J], F32, name="picked1", align_bytes=64, offset=Y)
+        nc.vector.tensor_copy(picked1[:], carried1[:].indirect(offsets[:]))
+
+        def tab_operand(a, jt):
+            codes = tab_codes[:, a, 2 * jt * J_TILE : 2 * (jt + 1) * J_TILE].bitcast(FP4X4)
+            return codes, tab_planes[:, a, jt * J_TILE : (jt + 1) * J_TILE]
+
+        gates, carries = [], []
         for c in range(N_TILES):
-            gate = keep.tile([P, J], F32, name="gate%d" % c, align_bytes=64)
-            rest = keep.tile([P, J], F32, name="rest%d" % c, align_bytes=64)
+            gate = keep.tile([P, J], F32, name="gate%d" % c, align_bytes=64, tag="gate%d" % c)
+            carry = keep.tile([P, J], F32, name="carry%d" % c, align_bytes=64)
             for jt in range(J_TILES):
                 cols = slice(jt * J_TILE, (jt + 1) * J_TILE)
                 acc = psum.tile([P, J_TILE], F32, name="ga%d%d" % (c, jt))
@@ -143,32 +174,45 @@ def tile_list_hwayt_hl_relu_kernel(
                         start=(a == 0),
                         stop=(a == PASSES - 1),
                     )
-                nc.scalar.activation(gate[:, cols], acc[:], ACT.Sigmoid, bias=bias[:, c : c + 1])
-                nc.scalar.activation(rest[:, cols], gate[:, cols], ACT.Copy, bias=1.0, scale=-1.0)
+                nc.scalar.activation(carry[:, cols], acc[:], ACT.Sigmoid, bias=minus_bias[:, c : c + 1], scale=-1.0)
+            nc.scalar.activation(gate[:], carry[:], ACT.Copy, bias=1.0, scale=-1.0)
             gates.append(gate)
-            kept.append(rest)
+            carries.append(carry)
 
-        for c in range(N_TILES):
-            stay = keep.tile([P, J], F32, name="stay%d" % c, align_bytes=64)
-            nc.vector.tensor_tensor(stay[:], carried[c][:].indirect(offsets[:]), kept[c][:], ALU.mult)
-            for jt in range(J_TILES):
-                cols = slice(jt * J_TILE, (jt + 1) * J_TILE)
-                acc = psum.tile([P, J_TILE], F32, name="ha%d%d" % (c, jt))
-                steps = [(a, h) for a in range(PASSES) for h in range(2)]
-                for s, (a, h) in enumerate(steps):
-                    codes, plane = tab_operand(a, jt)
+        blocks = [(c, jt) for c in range(N_TILES) for jt in range(J_TILES)]
+        ha = {}
+        for c, jt in blocks:
+            ha[c, jt] = psum.tile([P, J_TILE], F32, name="ha%d%d" % (c, jt))
+        for a in range(PASSES):
+            for c, jt in blocks:
+                codes, plane = tab_operand(a, jt)
+                for h in range(2):
                     wcols = slice(h * N + c * P, h * N + (c + 1) * P)
                     nc.tensor.matmul_mx(
-                        out=acc[:],
+                        out=ha[c, jt][:],
                         lhsT=wh_codes[a][:, wcols].bitcast(FP8X4),
                         lhsT_scale=wh_planes[a][:, wcols],
                         rhs=codes,
                         rhs_scale=plane,
-                        start=(s == 0),
-                        stop=(s == len(steps) - 1),
+                        start=(a == 0 and h == 0),
+                        stop=(a == PASSES - 1 and h == 1),
                     )
-                made = keep.tile([P, J_TILE], F32, name="made%d%d" % (c, jt), align_bytes=64)
-                nc.vector.scalar_tensor_tensor(made[:], acc[:], 0.0, gates[c][:, cols], ALU.max, ALU.mult)
-                result = keep.tile([P, J_TILE], F32, name="result%d%d" % (c, jt), align_bytes=64)
-                nc.vector.tensor_tensor(result[:], made[:], stay[:, cols], ALU.add)
-                nc.sync.dma_start(out=out[c * P : (c + 1) * P, cols], in_=result[:])
+
+        stay0 = reuse.tile([P, J], F32, name="stay0", align_bytes=64, offset=Y + 4 * KB)
+        nc.gpsimd.tensor_tensor(stay0[:], picked0[:], carries[0][:], ALU.mult)
+        stay1 = keep.tile([P, J], F32, name="stay1", align_bytes=64)
+        nc.gpsimd.tensor_tensor(stay1[:], picked1[:], carries[1][:], ALU.mult)
+
+        made = reuse.tile([P, N_TILES, J], F32, name="made", align_bytes=64, offset=0)
+        for c, jt in blocks:
+            cols = slice(jt * J_TILE, (jt + 1) * J_TILE)
+            nc.vector.scalar_tensor_tensor(made[:, c, cols], ha[c, jt][:], 0.0, gates[c][:, cols], ALU.max, ALU.mult)
+
+        result0 = keep.tile([P, J], F32, name="result0", align_bytes=64, tag="gate1")
+        nc.vector.tensor_tensor(result0[:], made[:, 0, :], stay0[:], ALU.add)
+        nc.sync.dma_start(out=out[0:P, :], in_=result0[:])
+        edges = [0, J_TILE, J_TILE + J_TILE // 2, J]
+        for lo, hi in zip(edges, edges[1:]):
+            result = keep.tile([P, hi - lo], F32, name="result1_%d" % lo, align_bytes=64)
+            nc.vector.tensor_tensor(result[:], made[:, 1, lo:hi], stay1[:, lo:hi], ALU.add)
+            nc.sync.dma_start(out=out[P : 2 * P, lo:hi], in_=result[:])

@@ -22,13 +22,18 @@ PASSES = K // (P * PACK)
 N_TILES = N // P
 J_TILE = 512
 J_TILES = J // J_TILE
-QUADS = 4
 QUAD = 32
+QUADS = P // QUAD
+ROWS = 4
+FIRST_ROW = QUAD - PASSES * ROWS
+PLANE_SPAN = P - QUAD + ROWS
 HI_MASK = 0xFFF0FFF0 - (1 << 32)
-LIVE = 24
-SPAN = 100
+
 KB = 1024
-Y = 8 * KB
+AT_WINDOW = 0
+AT_PICKED1 = 8 * KB
+AT_PARTS = 10 * KB
+AT_KEPT0 = 12 * KB
 
 
 def tile_list_hwayt_hl_relu_kernel(
@@ -37,35 +42,31 @@ def tile_list_hwayt_hl_relu_kernel(
     nc = tc.nc
     with ExitStack() as ctx:
         keep = ctx.enter_context(tc.tile_pool(name="keep", bufs=1))
-        reuse = ctx.enter_context(tc.tile_pool(name="reuse", bufs=1))
+        shared = ctx.enter_context(tc.tile_pool(name="shared", bufs=1))
         psum = ctx.enter_context(tc.psum_pool(name="psum", bufs=1))
 
         offsets = keep.tile([P, J // 16], U16, name="offsets")
         nc.sync.dma_start(offsets[:], offs)
 
-        scale_rows = reuse.tile([P, T], U8, name="scale_rows", align_bytes=64, offset=0)
+        scale_rows = shared.tile([P, T], U8, name="scale_rows", align_bytes=64, offset=AT_WINDOW)
         for q in range(QUADS):
             nc.sync.dma_start(
-                out=scale_rows[QUAD * q + LIVE : QUAD * (q + 1), :].bitcast(I32),
-                in_=tab_scales[:, 4 * q : 4 * q + 4, :].bitcast(I32),
+                out=scale_rows[QUAD * q + FIRST_ROW : QUAD * (q + 1), :].bitcast(I32),
+                in_=tab_scales[:, ROWS * q : ROWS * (q + 1), :].bitcast(I32),
             )
         for q in range(QUADS):
-            nc.vector.memset(scale_rows[QUAD * q : QUAD * q + LIVE, :].bitcast(I32), 0)
+            nc.vector.memset(scale_rows[QUAD * q : QUAD * q + FIRST_ROW, :].bitcast(I32), 0)
 
-        def load_wh(a, raw):
+        def load_wh(a):
+            raw = keep.tile([P, PACK, N], F32, name="wh_raw%d" % a, align_bytes=64)
             rows = wh[a * P * PACK : (a + 1) * P * PACK, :]
             nc.sync.dma_start(out=raw[:], in_=rows.rearrange("(p i) n -> p i n", i=PACK))
+            return raw
 
-        wh_raw = [
-            keep.tile([P, PACK, N], F32, name="wh_raw0", align_bytes=64),
-            keep.tile([P, PACK, N], F32, name="wh_raw1", align_bytes=64),
-        ]
-        load_wh(0, wh_raw[0])
+        wh_raw0 = load_wh(0)
         words = keep.tile([P, T], U32, name="words", align_bytes=64)
-        nc.sync.dma_start(
-            out=words[:].bitcast(I32), in_=tab_words[0].rearrange("p t b -> p (t b)").bitcast(I32)
-        )
-        load_wh(1, wh_raw[1])
+        nc.sync.dma_start(out=words[:].bitcast(I32), in_=tab_words[0].rearrange("p t b -> p (t b)").bitcast(I32))
+        wh_raw1 = load_wh(1)
 
         bias = keep.tile([P, N_TILES], F32, name="bias")
         with nc.allow_non_contiguous_dma(reason="one bias value for each partition"):
@@ -78,40 +79,41 @@ def tile_list_hwayt_hl_relu_kernel(
         nc.gpsimd.memset(wg_planes[:].bitcast(I32), 0)
         for q in range(QUADS):
             nc.sync.dma_start(
-                out=wg_planes[QUAD * q : QUAD * q + 4, :, :].bitcast(I32),
-                in_=wg_scales[:, 4 * q : 4 * q + 4, :].rearrange("a r n -> r a n").bitcast(I32),
+                out=wg_planes[QUAD * q : QUAD * q + ROWS, :, :].bitcast(I32),
+                in_=wg_scales[:, ROWS * q : ROWS * (q + 1), :].rearrange("a r n -> r a n").bitcast(I32),
             )
-        carried0 = keep.tile([P, T], F32, name="carried0", align_bytes=64, tag="codes1")
-        nc.sync.dma_start(out=carried0[:], in_=rT[0:P, :])
+        r_rows0 = keep.tile([P, T], F32, name="r_rows0", align_bytes=64, tag="codes1")
+        nc.sync.dma_start(out=r_rows0[:], in_=rT[0:P, :])
 
         tab_planes = keep.tile([P, PASSES, J], U8, name="tab_planes", align_bytes=64)
         nc.vector.memset(tab_planes[P - QUAD : P, :, :].bitcast(I32), 0)
 
         warm = keep.tile([P, N_TILES], F32, name="warm")
-        seed = keep.tile([P, N_TILES], F32, name="seed")
-        nc.gpsimd.memset(seed[:], 0.0)
-        nc.scalar.activation(warm[:], seed[:], ACT.Sigmoid)
+        zeros = keep.tile([P, N_TILES], F32, name="zeros")
+        nc.gpsimd.memset(zeros[:], 0.0)
+        nc.scalar.activation(warm[:], zeros[:], ACT.Sigmoid)
         minus_bias = keep.tile([P, N_TILES], F32, name="minus_bias")
         nc.scalar.activation(minus_bias[:], bias[:], ACT.Copy, scale=-1.0)
 
         picked_scales = keep.tile([P, J], U8, name="picked_scales", align_bytes=64)
         nc.vector.tensor_copy(picked_scales[:], scale_rows[:].indirect(offsets[:]))
         for a in range(PASSES):
-            first = LIVE + 4 * a
+            first = FIRST_ROW + ROWS * a
             nc.sync.dma_start(
-                out=tab_planes[0:SPAN, a, :].bitcast(I32), in_=picked_scales[first : first + SPAN, :].bitcast(I32)
+                out=tab_planes[0:PLANE_SPAN, a, :].bitcast(I32),
+                in_=picked_scales[first : first + PLANE_SPAN, :].bitcast(I32),
             )
 
-        carried1 = reuse.tile([P, T], F32, name="carried1", align_bytes=64, offset=0)
-        nc.sync.dma_start(out=carried1[:], in_=rT[P : 2 * P, :])
+        r_rows1 = shared.tile([P, T], F32, name="r_rows1", align_bytes=64, offset=AT_WINDOW)
+        nc.sync.dma_start(out=r_rows1[:], in_=rT[P : 2 * P, :])
 
-        def split(a):
+        def split(a, raw):
             upper = keep.tile([P, N, PACK], BF16, name="upper%d" % a, align_bytes=64, tag="upper%d" % a)
-            halves = wh_raw[a][:].bitcast(BF16).rearrange("p i (n e) -> p n i e", e=2)
+            halves = raw[:].bitcast(BF16).rearrange("p i (n e) -> p n i e", e=2)
             nc.scalar.copy(out=upper[:], in_=halves[:, :, :, 1])
             woven = keep.tile([P, N, PACK], F32, name="woven%d" % a, align_bytes=64)
-            nc.scalar.copy(out=woven[:], in_=wh_raw[a][:].rearrange("p i n -> p n i"))
-            parts = reuse.tile([P, 2, N * PACK], BF16, name="parts%d" % a, align_bytes=64, offset=Y + 2 * KB)
+            nc.scalar.copy(out=woven[:], in_=raw[:].rearrange("p i n -> p n i"))
+            parts = shared.tile([P, 2, N * PACK], BF16, name="parts%d" % a, align_bytes=64, offset=AT_PARTS)
             nc.vector.tensor_scalar(
                 parts[:, 0, :].bitcast(I32),
                 upper[:].rearrange("p n i -> p (n i)").bitcast(I32),
@@ -124,57 +126,56 @@ def tile_list_hwayt_hl_relu_kernel(
             )
             return parts
 
-        wh_codes, wh_planes = [], []
-
         def quantise(a, parts):
             codes = keep.tile([P, 2 * N], U32, name="wh_codes%d" % a, align_bytes=64, tag="codes%d" % a)
-            planes = keep.tile([P, 2 * N], U8, name="wh_planes%d" % a, align_bytes=64)
+            plane = keep.tile([P, 2 * N], U8, name="wh_plane%d" % a, align_bytes=64)
             nc.vector.quantize_mx(
-                out=codes[:].bitcast(FP8X4), scales=planes[:], in_=parts[:].rearrange("p h x -> p (h x)")
+                out=codes[:].bitcast(FP8X4), scales=plane[:], in_=parts[:].rearrange("p h x -> p (h x)")
             )
-            wh_codes.append(codes)
-            wh_planes.append(planes)
+            return codes, plane
 
-        parts0 = split(0)
-
+        parts0 = split(0, wh_raw0)
         picked_words = keep.tile([P, J], U32, name="picked_words", align_bytes=64, tag="upper0")
         nc.vector.tensor_copy(picked_words[:], words[:].indirect(offsets[:]))
         tab_codes = keep.tile([P, PASSES, 2 * J], U8, name="tab_codes", align_bytes=64)
         nc.vector.tensor_copy(
-            tab_codes[:].bitcast(U16), picked_words[:].bitcast(U16).rearrange("p (j d) -> p d j", d=PASSES)
+            tab_codes[:].bitcast(U16), picked_words[:].bitcast(U16).rearrange("p (j a) -> p a j", a=PASSES)
         )
-        quantise(0, parts0)
+        wh_pass0 = quantise(0, parts0)
 
-        parts1 = split(1)
-        picked0 = keep.tile([P, J], F32, name="picked0", align_bytes=64, tag="upper1")
-        nc.vector.tensor_copy(picked0[:], carried0[:].indirect(offsets[:]))
-        quantise(1, parts1)
-        picked1 = reuse.tile([P, J], F32, name="picked1", align_bytes=64, offset=Y)
-        nc.vector.tensor_copy(picked1[:], carried1[:].indirect(offsets[:]))
+        parts1 = split(1, wh_raw1)
+        r_picked0 = keep.tile([P, J], F32, name="r_picked0", align_bytes=64, tag="upper1")
+        nc.vector.tensor_copy(r_picked0[:], r_rows0[:].indirect(offsets[:]))
+        wh_pass1 = quantise(1, parts1)
+        r_picked1 = shared.tile([P, J], F32, name="r_picked1", align_bytes=64, offset=AT_PICKED1)
+        nc.vector.tensor_copy(r_picked1[:], r_rows1[:].indirect(offsets[:]))
 
-        def tab_operand(a, jt):
-            codes = tab_codes[:, a, 2 * jt * J_TILE : 2 * (jt + 1) * J_TILE].bitcast(FP4X4)
-            return codes, tab_planes[:, a, jt * J_TILE : (jt + 1) * J_TILE]
+        def columns(jt):
+            return slice(jt * J_TILE, (jt + 1) * J_TILE)
+
+        def multiply(acc, weights, weight_plane, a, jt, start, stop):
+            nc.tensor.matmul_mx(
+                out=acc[:],
+                lhsT=weights,
+                lhsT_scale=weight_plane,
+                rhs=tab_codes[:, a, 2 * jt * J_TILE : 2 * (jt + 1) * J_TILE].bitcast(FP4X4),
+                rhs_scale=tab_planes[:, a, columns(jt)],
+                start=start,
+                stop=stop,
+            )
 
         gates, carries = [], []
         for c in range(N_TILES):
             gate = keep.tile([P, J], F32, name="gate%d" % c, align_bytes=64, tag="gate%d" % c)
             carry = keep.tile([P, J], F32, name="carry%d" % c, align_bytes=64)
             for jt in range(J_TILES):
-                cols = slice(jt * J_TILE, (jt + 1) * J_TILE)
-                acc = psum.tile([P, J_TILE], F32, name="ga%d%d" % (c, jt))
+                ga = psum.tile([P, J_TILE], F32, name="ga%d%d" % (c, jt))
                 for a in range(PASSES):
-                    codes, plane = tab_operand(a, jt)
-                    nc.tensor.matmul_mx(
-                        out=acc[:],
-                        lhsT=wg_codes[:, a, 2 * c * P : 2 * (c + 1) * P].bitcast(FP4X4),
-                        lhsT_scale=wg_planes[:, a, c * P : (c + 1) * P],
-                        rhs=codes,
-                        rhs_scale=plane,
-                        start=(a == 0),
-                        stop=(a == PASSES - 1),
-                    )
-                nc.scalar.activation(carry[:, cols], acc[:], ACT.Sigmoid, bias=minus_bias[:, c : c + 1], scale=-1.0)
+                    weights = wg_codes[:, a, 2 * c * P : 2 * (c + 1) * P].bitcast(FP4X4)
+                    multiply(ga, weights, wg_planes[:, a, c * P : (c + 1) * P], a, jt, a == 0, a == PASSES - 1)
+                nc.scalar.activation(
+                    carry[:, columns(jt)], ga[:], ACT.Sigmoid, bias=minus_bias[:, c : c + 1], scale=-1.0
+                )
             nc.scalar.activation(gate[:], carry[:], ACT.Copy, bias=1.0, scale=-1.0)
             gates.append(gate)
             carries.append(carry)
@@ -183,36 +184,30 @@ def tile_list_hwayt_hl_relu_kernel(
         ha = {}
         for c, jt in blocks:
             ha[c, jt] = psum.tile([P, J_TILE], F32, name="ha%d%d" % (c, jt))
-        for a in range(PASSES):
+        for a, (codes, plane) in enumerate([wh_pass0, wh_pass1]):
             for c, jt in blocks:
-                codes, plane = tab_operand(a, jt)
-                for h in range(2):
-                    wcols = slice(h * N + c * P, h * N + (c + 1) * P)
-                    nc.tensor.matmul_mx(
-                        out=ha[c, jt][:],
-                        lhsT=wh_codes[a][:, wcols].bitcast(FP8X4),
-                        lhsT_scale=wh_planes[a][:, wcols],
-                        rhs=codes,
-                        rhs_scale=plane,
-                        start=(a == 0 and h == 0),
-                        stop=(a == PASSES - 1 and h == 1),
-                    )
+                for part in range(2):
+                    own = slice(part * N + c * P, part * N + (c + 1) * P)
+                    start, stop = (a, part) == (0, 0), (a, part) == (PASSES - 1, 1)
+                    multiply(ha[c, jt], codes[:, own].bitcast(FP8X4), plane[:, own], a, jt, start, stop)
 
-        stay0 = reuse.tile([P, J], F32, name="stay0", align_bytes=64, offset=Y + 4 * KB)
-        nc.gpsimd.tensor_tensor(stay0[:], picked0[:], carries[0][:], ALU.mult)
-        stay1 = keep.tile([P, J], F32, name="stay1", align_bytes=64)
-        nc.gpsimd.tensor_tensor(stay1[:], picked1[:], carries[1][:], ALU.mult)
+        kept0 = shared.tile([P, J], F32, name="kept0", align_bytes=64, offset=AT_KEPT0)
+        nc.gpsimd.tensor_tensor(kept0[:], r_picked0[:], carries[0][:], ALU.mult)
+        kept1 = keep.tile([P, J], F32, name="kept1", align_bytes=64)
+        nc.gpsimd.tensor_tensor(kept1[:], r_picked1[:], carries[1][:], ALU.mult)
 
-        made = reuse.tile([P, N_TILES, J], F32, name="made", align_bytes=64, offset=0)
+        made = shared.tile([P, N_TILES, J], F32, name="made", align_bytes=64, offset=AT_WINDOW)
         for c, jt in blocks:
-            cols = slice(jt * J_TILE, (jt + 1) * J_TILE)
-            nc.vector.scalar_tensor_tensor(made[:, c, cols], ha[c, jt][:], 0.0, gates[c][:, cols], ALU.max, ALU.mult)
+            nc.vector.scalar_tensor_tensor(
+                made[:, c, columns(jt)], ha[c, jt][:], 0.0, gates[c][:, columns(jt)], ALU.max, ALU.mult
+            )
 
         result0 = keep.tile([P, J], F32, name="result0", align_bytes=64, tag="gate1")
-        nc.vector.tensor_tensor(result0[:], made[:, 0, :], stay0[:], ALU.add)
-        nc.sync.dma_start(out=out[0:P, :], in_=result0[:])
+        for jt in range(J_TILES):
+            nc.vector.tensor_tensor(result0[:, columns(jt)], made[:, 0, columns(jt)], kept0[:, columns(jt)], ALU.add)
+            nc.sync.dma_start(out=out[0:P, columns(jt)], in_=result0[:, columns(jt)])
         edges = [0, J_TILE, J_TILE + J_TILE // 2, J]
         for lo, hi in zip(edges, edges[1:]):
-            result = keep.tile([P, hi - lo], F32, name="result1_%d" % lo, align_bytes=64)
-            nc.vector.tensor_tensor(result[:], made[:, 1, lo:hi], stay1[:, lo:hi], ALU.add)
-            nc.sync.dma_start(out=out[P : 2 * P, lo:hi], in_=result[:])
+            result1 = keep.tile([P, hi - lo], F32, name="result1_%d" % lo, align_bytes=64)
+            nc.vector.tensor_tensor(result1[:], made[:, 1, lo:hi], kept1[:, lo:hi], ALU.add)
+            nc.sync.dma_start(out=out[P : 2 * P, lo:hi], in_=result1[:])

@@ -25,15 +25,27 @@ J_TILES = J // J_TILE
 QUAD = 32
 QUADS = P // QUAD
 ROWS = 4
-FIRST_ROW = QUAD - PASSES * ROWS
-PLANE_SPAN = P - QUAD + ROWS
-HI_MASK = 0xFFF0FFF0 - (1 << 32)
+SHIFT = 16
+WORD_MASK = 0xFFF00000 - (1 << 32)
+PAIR_MASK = 0xFFF0FFF0 - (1 << 32)
 
 KB = 1024
-AT_WINDOW = 0
-AT_PICKED1 = 8 * KB
-AT_PARTS = 10 * KB
-AT_KEPT0 = 12 * KB
+AT_WINDOW = 8 * KB
+AT_R1 = KB // 2
+AT_WG = 8 * KB + KB // 2
+AT_BIAS = 9 * KB + KB // 2
+AT_R0 = 9 * KB + 3 * KB // 4
+AT_PICKED1 = 18 * KB
+AT_PARTS = 20 * KB
+AT_LOST0 = 22 * KB
+AT_RAW = (30 * KB, 34 * KB)
+AT_WOVEN = (38 * KB, 42 * KB)
+AT_PICKED0 = 36 * KB
+AT_PICKED_WORDS = 26 * KB
+
+
+def columns(jt):
+    return slice(jt * J_TILE, (jt + 1) * J_TILE)
 
 
 def tile_list_hwayt_hl_relu_kernel(
@@ -49,16 +61,20 @@ def tile_list_hwayt_hl_relu_kernel(
         nc.sync.dma_start(offsets[:], offs)
 
         scale_rows = shared.tile([P, T], U8, name="scale_rows", align_bytes=64, offset=AT_WINDOW)
-        for q in range(QUADS):
+        nc.gpsimd.memset(scale_rows[:].bitcast(I32), 0)
+        bias = keep.tile([P, N_TILES], F32, name="bias")
+        with nc.allow_non_contiguous_dma(reason="one bias value for each partition"):
+            nc.sync.dma_start(out=bias[:], in_=bg.rearrange("(c p) -> p c", p=P))
+        wg_codes = keep.tile([P, PASSES, 2 * N], U8, name="wg_codes", align_bytes=64)
+        nc.sync.dma_start(out=wg_codes[:].bitcast(I32), in_=wg_words.rearrange("a p b -> p a b").bitcast(I32))
+        for r in range(ROWS):
             nc.sync.dma_start(
-                out=scale_rows[QUAD * q + FIRST_ROW : QUAD * (q + 1), :].bitcast(I32),
-                in_=tab_scales[:, ROWS * q : ROWS * (q + 1), :].bitcast(I32),
+                out=scale_rows[r:P:SHIFT, :].bitcast(I32),
+                in_=tab_scales[:, r : QUADS * ROWS : ROWS, :].rearrange("a q t -> q a t").bitcast(I32),
             )
-        for q in range(QUADS):
-            nc.vector.memset(scale_rows[QUAD * q : QUAD * q + FIRST_ROW, :].bitcast(I32), 0)
 
         def load_wh(a):
-            raw = keep.tile([P, PACK, N], F32, name="wh_raw%d" % a, align_bytes=64)
+            raw = shared.tile([P, PACK, N], F32, name="wh_raw%d" % a, align_bytes=64, offset=AT_RAW[a])
             rows = wh[a * P * PACK : (a + 1) * P * PACK, :]
             nc.sync.dma_start(out=raw[:], in_=rows.rearrange("(p i) n -> p i n", i=PACK))
             return raw
@@ -68,13 +84,6 @@ def tile_list_hwayt_hl_relu_kernel(
         nc.sync.dma_start(out=words[:].bitcast(I32), in_=tab_words[0].rearrange("p t b -> p (t b)").bitcast(I32))
         wh_raw1 = load_wh(1)
 
-        bias = keep.tile([P, N_TILES], F32, name="bias")
-        with nc.allow_non_contiguous_dma(reason="one bias value for each partition"):
-            nc.sync.dma_start(out=bias[:], in_=bg.rearrange("(c p) -> p c", p=P))
-
-        wg_codes = keep.tile([P, PASSES, 2 * N], U8, name="wg_codes", align_bytes=64)
-        nc.sync.dma_start(out=wg_codes[:].bitcast(I32), in_=wg_words.rearrange("a p b -> p a b").bitcast(I32))
-
         wg_planes = keep.tile([P, PASSES, N], U8, name="wg_planes", align_bytes=64)
         nc.gpsimd.memset(wg_planes[:].bitcast(I32), 0)
         for q in range(QUADS):
@@ -82,132 +91,136 @@ def tile_list_hwayt_hl_relu_kernel(
                 out=wg_planes[QUAD * q : QUAD * q + ROWS, :, :].bitcast(I32),
                 in_=wg_scales[:, ROWS * q : ROWS * (q + 1), :].rearrange("a r n -> r a n").bitcast(I32),
             )
-        r_rows0 = keep.tile([P, T], F32, name="r_rows0", align_bytes=64, tag="codes1")
-        nc.sync.dma_start(out=r_rows0[:], in_=rT[0:P, :])
 
-        tab_planes = keep.tile([P, PASSES, J], U8, name="tab_planes", align_bytes=64)
-        nc.vector.memset(tab_planes[P - QUAD : P, :, :].bitcast(I32), 0)
-
-        warm = keep.tile([P, N_TILES], F32, name="warm")
-        zeros = keep.tile([P, N_TILES], F32, name="zeros")
-        nc.gpsimd.memset(zeros[:], 0.0)
-        nc.scalar.activation(warm[:], zeros[:], ACT.Sigmoid)
-        minus_bias = keep.tile([P, N_TILES], F32, name="minus_bias")
-        nc.scalar.activation(minus_bias[:], bias[:], ACT.Copy, scale=-1.0)
+        tab_plane1 = keep.tile([P, J], U8, name="tab_plane1", align_bytes=64)
+        nc.vector.memset(tab_plane1[P - QUAD : P, :].bitcast(I32), 0)
 
         picked_scales = keep.tile([P, J], U8, name="picked_scales", align_bytes=64)
         nc.vector.tensor_copy(picked_scales[:], scale_rows[:].indirect(offsets[:]))
-        for a in range(PASSES):
-            first = FIRST_ROW + ROWS * a
-            nc.sync.dma_start(
-                out=tab_planes[0:PLANE_SPAN, a, :].bitcast(I32),
-                in_=picked_scales[first : first + PLANE_SPAN, :].bitcast(I32),
-            )
+        nc.sync.dma_start(out=tab_plane1[0 : P - SHIFT, :].bitcast(I32), in_=picked_scales[SHIFT:P, :].bitcast(I32))
+        tab_planes = [picked_scales, tab_plane1]
 
-        r_rows1 = shared.tile([P, T], F32, name="r_rows1", align_bytes=64, offset=AT_WINDOW)
+        r_rows0 = shared.tile([P, T], F32, name="r_rows0", align_bytes=64, offset=AT_R0)
+        nc.sync.dma_start(out=r_rows0[:], in_=rT[0:P, :])
+        r_rows1 = shared.tile([P, T], F32, name="r_rows1", align_bytes=64, offset=AT_R1)
         nc.sync.dma_start(out=r_rows1[:], in_=rT[P : 2 * P, :])
 
-        def split(a, raw):
-            upper = keep.tile([P, N, PACK], BF16, name="upper%d" % a, align_bytes=64, tag="upper%d" % a)
-            halves = raw[:].bitcast(BF16).rearrange("p i (n e) -> p n i e", e=2)
-            nc.scalar.copy(out=upper[:], in_=halves[:, :, :, 1])
-            woven = keep.tile([P, N, PACK], F32, name="woven%d" % a, align_bytes=64)
-            nc.scalar.copy(out=woven[:], in_=raw[:].rearrange("p i n -> p n i"))
-            parts = shared.tile([P, 2, N * PACK], BF16, name="parts%d" % a, align_bytes=64, offset=AT_PARTS)
-            nc.vector.tensor_scalar(
-                parts[:, 0, :].bitcast(I32),
-                upper[:].rearrange("p n i -> p (n i)").bitcast(I32),
-                HI_MASK,
-                None,
-                ALU.bitwise_and,
-            )
-            nc.gpsimd.tensor_tensor(
-                parts[:, 1, :], woven[:].rearrange("p n i -> p (n i)"), parts[:, 0, :], ALU.subtract
-            )
-            return parts
+        def weave(a, raw):
+            woven = shared.tile([P, N * PACK], F32, name="woven%d" % a, align_bytes=64, offset=AT_WOVEN[a])
+            nc.scalar.copy(out=woven[:].rearrange("p (n i) -> p n i", i=PACK), in_=raw[:].rearrange("p i n -> p n i"))
+            return woven
 
-        def quantise(a, parts):
-            codes = keep.tile([P, 2 * N], U32, name="wh_codes%d" % a, align_bytes=64, tag="codes%d" % a)
-            plane = keep.tile([P, 2 * N], U8, name="wh_plane%d" % a, align_bytes=64)
-            nc.vector.quantize_mx(
-                out=codes[:].bitcast(FP8X4), scales=plane[:], in_=parts[:].rearrange("p h x -> p (h x)")
-            )
-            return codes, plane
 
-        parts0 = split(0, wh_raw0)
-        picked_words = keep.tile([P, J], U32, name="picked_words", align_bytes=64, tag="upper0")
-        nc.vector.tensor_copy(picked_words[:], words[:].indirect(offsets[:]))
-        tab_codes = keep.tile([P, PASSES, 2 * J], U8, name="tab_codes", align_bytes=64)
-        nc.vector.tensor_copy(
-            tab_codes[:].bitcast(U16), picked_words[:].bitcast(U16).rearrange("p (j a) -> p a j", a=PASSES)
+        woven0 = weave(0, wh_raw0)
+        hi0 = keep.tile([P, N * PACK], F32, name="hi0", align_bytes=64)
+        word_mask = shared.tile([P, 1], I32, name="word_mask", align_bytes=64, offset=AT_PICKED_WORDS)
+        nc.gpsimd.memset(word_mask[:], WORD_MASK)
+        nc.vector.tensor_scalar(hi0[:].bitcast(I32), woven0[:].bitcast(I32), word_mask[:], None, ALU.bitwise_and)
+        parts0 = shared.tile([P, 2, N * PACK], BF16, name="parts0", align_bytes=64, offset=AT_PARTS)
+        nc.gpsimd.tensor_tensor(parts0[:, 1, :], woven0[:], hi0[:], ALU.subtract)
+        nc.scalar.copy(out=parts0[:, 0, :], in_=hi0[:])
+
+        picked_words = shared.tile([P, J], U32, name="picked_words", align_bytes=64, offset=AT_PICKED_WORDS)
+        for jt in range(J_TILES):
+            entries = offsets[:, jt * J_TILE // 16 : (jt + 1) * J_TILE // 16]
+            nc.vector.tensor_copy(picked_words[:, columns(jt)], words[:].indirect(entries))
+        tab_codes = []
+        for jt in range(J_TILES):
+            codes = keep.tile([P, PASSES, 2 * J_TILE], U8, name="tab_codes%d" % jt, align_bytes=64)
+            nc.vector.tensor_copy(
+                codes[:].bitcast(U16),
+                picked_words[:, columns(jt)].bitcast(U16).rearrange("p (j a) -> p a j", a=PASSES),
+            )
+            tab_codes.append(codes)
+        wh_codes0 = keep.tile([P, 2 * N], U32, name="wh_codes0", align_bytes=64)
+        wh_plane0 = keep.tile([P, 2 * N], U8, name="wh_plane0", align_bytes=64)
+        nc.vector.quantize_mx(
+            out=wh_codes0[:].bitcast(FP8X4), scales=wh_plane0[:], in_=parts0[:].rearrange("p h x -> p (h x)")
         )
-        wh_pass0 = quantise(0, parts0)
 
-        parts1 = split(1, wh_raw1)
-        r_picked0 = keep.tile([P, J], F32, name="r_picked0", align_bytes=64, tag="upper1")
+        upper1 = keep.tile([P, N, PACK], BF16, name="upper1", align_bytes=64)
+        halves = wh_raw1[:].bitcast(BF16).rearrange("p i (n e) -> p n i e", e=2)
+        nc.scalar.copy(out=upper1[:], in_=halves[:, :, :, 1])
+        woven1 = weave(1, wh_raw1)
+        hi1 = keep.tile([P, N * PACK], BF16, name="hi1", align_bytes=64)
+        nc.vector.tensor_scalar(
+            hi1[:].bitcast(I32), upper1[:].rearrange("p n i -> p (n i)").bitcast(I32), PAIR_MASK, None, ALU.bitwise_and
+        )
+        lo1 = shared.tile([P, N * PACK], BF16, name="lo1", align_bytes=64, offset=AT_PARTS)
+        nc.gpsimd.tensor_tensor(lo1[:], woven1[:], hi1[:], ALU.subtract)
+
+        r_picked0 = shared.tile([P, J], F32, name="r_picked0", align_bytes=64, offset=AT_PICKED0)
         nc.vector.tensor_copy(r_picked0[:], r_rows0[:].indirect(offsets[:]))
-        wh_pass1 = quantise(1, parts1)
-        r_picked1 = shared.tile([P, J], F32, name="r_picked1", align_bytes=64, offset=AT_PICKED1)
+        hi_codes1 = shared.tile([P, N], U32, name="hi_codes1", align_bytes=64, offset=AT_R0)
+        lo_codes1 = shared.tile([P, N], U32, name="lo_codes1", align_bytes=64, offset=AT_R0 + KB)
+        wh_plane1 = keep.tile([P, 2 * N], U8, name="wh_plane1", align_bytes=64)
+        nc.vector.quantize_mx(out=hi_codes1[:].bitcast(FP8X4), scales=wh_plane1[:, 0:N], in_=hi1[:])
+        nc.vector.quantize_mx(out=lo_codes1[:].bitcast(FP8X4), scales=wh_plane1[:, N : 2 * N], in_=lo1[:])
+        r_picked1 = shared.tile([P, J], F32, name="r_picked1", align_bytes=64, offset=AT_WOVEN[1])
         nc.vector.tensor_copy(r_picked1[:], r_rows1[:].indirect(offsets[:]))
-
-        def columns(jt):
-            return slice(jt * J_TILE, (jt + 1) * J_TILE)
+        wh_codes = [[wh_codes0[:, 0:N], wh_codes0[:, N : 2 * N]], [hi_codes1[:], lo_codes1[:]]]
+        wh_planes = [wh_plane0, wh_plane1]
 
         def multiply(acc, weights, weight_plane, a, jt, start, stop):
             nc.tensor.matmul_mx(
                 out=acc[:],
                 lhsT=weights,
                 lhsT_scale=weight_plane,
-                rhs=tab_codes[:, a, 2 * jt * J_TILE : 2 * (jt + 1) * J_TILE].bitcast(FP4X4),
-                rhs_scale=tab_planes[:, a, columns(jt)],
+                rhs=tab_codes[jt][:, a, :].bitcast(FP4X4),
+                rhs_scale=tab_planes[a][:, columns(jt)],
                 start=start,
                 stop=stop,
             )
 
-        gates, carries = [], []
+        half_bias = keep.tile([P, N_TILES], F32, name="half_bias")
+        nc.scalar.activation(half_bias[:], bias[:], ACT.Copy, scale=0.5)
+        losses = []
         for c in range(N_TILES):
-            gate = keep.tile([P, J], F32, name="gate%d" % c, align_bytes=64, tag="gate%d" % c)
-            carry = keep.tile([P, J], F32, name="carry%d" % c, align_bytes=64)
+            tanh = keep.tile([P, J], F32, name="tanh%d" % c, align_bytes=64)
+            loss = keep.tile([P, J], F32, name="loss%d" % c, align_bytes=64, tag="loss%d" % c)
             for jt in range(J_TILES):
-                ga = psum.tile([P, J_TILE], F32, name="ga%d%d" % (c, jt))
-                for a in range(PASSES):
+                ga = psum.tile([P, J_TILE], F32, name="ga%d%d" % (c, jt), tag="bank%d%d" % (c, jt))
+                for a in reversed(range(PASSES)):
                     weights = wg_codes[:, a, 2 * c * P : 2 * (c + 1) * P].bitcast(FP4X4)
-                    multiply(ga, weights, wg_planes[:, a, c * P : (c + 1) * P], a, jt, a == 0, a == PASSES - 1)
+                    multiply(ga, weights, wg_planes[:, a, c * P : (c + 1) * P], a, jt, a == PASSES - 1, a == 0)
                 nc.scalar.activation(
-                    carry[:, columns(jt)], ga[:], ACT.Sigmoid, bias=minus_bias[:, c : c + 1], scale=-1.0
+                    tanh[:, columns(jt)], ga[:], ACT.Tanh, bias=half_bias[:, c : c + 1], scale=0.5
                 )
-            nc.scalar.activation(gate[:], carry[:], ACT.Copy, bias=1.0, scale=-1.0)
-            gates.append(gate)
-            carries.append(carry)
+                nc.scalar.activation(loss[:, columns(jt)], tanh[:, columns(jt)], ACT.Copy, bias=-0.5, scale=0.5)
+            losses.append(loss)
 
-        blocks = [(c, jt) for c in range(N_TILES) for jt in range(J_TILES)]
         ha = {}
-        for c, jt in blocks:
-            ha[c, jt] = psum.tile([P, J_TILE], F32, name="ha%d%d" % (c, jt))
-        for a, (codes, plane) in enumerate([wh_pass0, wh_pass1]):
-            for c, jt in blocks:
-                for part in range(2):
-                    own = slice(part * N + c * P, part * N + (c + 1) * P)
-                    start, stop = (a, part) == (0, 0), (a, part) == (PASSES - 1, 1)
-                    multiply(ha[c, jt], codes[:, own].bitcast(FP8X4), plane[:, own], a, jt, start, stop)
+        for c in range(N_TILES):
+            for jt in range(J_TILES):
+                ha[c, jt] = psum.tile([P, J_TILE], F32, name="ha%d%d" % (c, jt), tag="bank%d%d" % (c, jt))
+            for a in range(PASSES):
+                for jt in range(J_TILES):
+                    for part in range(2):
+                        codes = wh_codes[a][part][:, c * P : (c + 1) * P].bitcast(FP8X4)
+                        plane = wh_planes[a][:, part * N + c * P : part * N + (c + 1) * P]
+                        start, stop = (a, part) == (0, 0), (a, part) == (PASSES - 1, 1)
+                        multiply(ha[c, jt], codes, plane, a, jt, start, stop)
 
-        kept0 = shared.tile([P, J], F32, name="kept0", align_bytes=64, offset=AT_KEPT0)
-        nc.gpsimd.tensor_tensor(kept0[:], r_picked0[:], carries[0][:], ALU.mult)
-        kept1 = keep.tile([P, J], F32, name="kept1", align_bytes=64)
-        nc.gpsimd.tensor_tensor(kept1[:], r_picked1[:], carries[1][:], ALU.mult)
+        lost0 = shared.tile([P, J], F32, name="lost0", align_bytes=64, offset=AT_PARTS)
+        nc.gpsimd.tensor_tensor(lost0[:], r_picked0[:], losses[0][:], ALU.mult)
+        lost1 = keep.tile([P, J], F32, name="lost1", align_bytes=64)
+        nc.gpsimd.tensor_tensor(lost1[:], r_picked1[:], losses[1][:], ALU.mult)
 
-        made = shared.tile([P, N_TILES, J], F32, name="made", align_bytes=64, offset=AT_WINDOW)
-        for c, jt in blocks:
-            nc.vector.scalar_tensor_tensor(
-                made[:, c, columns(jt)], ha[c, jt][:], 0.0, gates[c][:, columns(jt)], ALU.max, ALU.mult
-            )
+        made = shared.tile([P, N_TILES, J], F32, name="made", align_bytes=64, offset=AT_R1)
+        for c in range(N_TILES):
+            for jt in range(J_TILES):
+                nc.vector.scalar_tensor_tensor(
+                    made[:, c, columns(jt)], losses[c][:, columns(jt)], 1.0, ha[c, jt][:], ALU.add, ALU.mult
+                )
 
-        result0 = keep.tile([P, J], F32, name="result0", align_bytes=64, tag="gate1")
+        result0 = keep.tile([P, J], F32, name="result0", align_bytes=64, tag="loss1")
         for jt in range(J_TILES):
-            nc.vector.tensor_tensor(result0[:, columns(jt)], made[:, 0, columns(jt)], kept0[:, columns(jt)], ALU.add)
+            nc.vector.scalar_tensor_tensor(
+                result0[:, columns(jt)], made[:, 0, columns(jt)], 0.0, lost0[:, columns(jt)], ALU.max, ALU.subtract
+            )
             nc.sync.dma_start(out=out[0:P, columns(jt)], in_=result0[:, columns(jt)])
         edges = [0, J_TILE, J_TILE + J_TILE // 2, J]
         for lo, hi in zip(edges, edges[1:]):
             result1 = keep.tile([P, hi - lo], F32, name="result1_%d" % lo, align_bytes=64)
-            nc.vector.tensor_tensor(result1[:], made[:, 1, lo:hi], kept1[:, lo:hi], ALU.add)
+            nc.vector.scalar_tensor_tensor(result1[:], made[:, 1, lo:hi], 0.0, lost1[:, lo:hi], ALU.max, ALU.subtract)
             nc.sync.dma_start(out=out[P : 2 * P, lo:hi], in_=result1[:])

@@ -25,6 +25,7 @@ J_TILES = J // J_TILE
 QUAD = 32
 QUADS = P // QUAD
 ROWS = 4
+STORE = 256
 SHIFT = 16
 WORD_MASK = 0xFFF00000 - (1 << 32)
 PAIR_MASK = 0xFFF0FFF0 - (1 << 32)
@@ -32,16 +33,10 @@ PAIR_MASK = 0xFFF0FFF0 - (1 << 32)
 KB = 1024
 AT_WINDOW = 8 * KB
 AT_R1 = KB // 2
-AT_WG = 8 * KB + KB // 2
-AT_BIAS = 9 * KB + KB // 2
-AT_R0 = 9 * KB + 3 * KB // 4
-AT_PICKED1 = 18 * KB
-AT_PARTS = 20 * KB
-AT_LOST0 = 22 * KB
-AT_RAW = (30 * KB, 34 * KB)
-AT_WOVEN = (38 * KB, 42 * KB)
-AT_PICKED0 = 36 * KB
+AT_R0 = 9 * KB + KB // 2
+AT_WORDS = 18 * KB
 AT_PICKED_WORDS = 26 * KB
+AT_PICKED0 = 30 * KB
 
 
 def columns(jt):
@@ -57,33 +52,33 @@ def tile_list_hwayt_hl_relu_kernel(
         shared = ctx.enter_context(tc.tile_pool(name="shared", bufs=1))
         psum = ctx.enter_context(tc.psum_pool(name="psum", bufs=1))
 
+        def entries(jt):
+            return offsets[:, jt * J_TILE // 16 : (jt + 1) * J_TILE // 16]
+
+        def load_wh(a):
+            raw = keep.tile([P, PACK, N], F32, name="wh_raw%d" % a, align_bytes=64)
+            rows = wh[a * P * PACK : (a + 1) * P * PACK, :]
+            nc.sync.dma_start(out=raw[:], in_=rows.rearrange("(p i) n -> p i n", i=PACK))
+            return raw
+
+        wh_raw0 = load_wh(0)
         offsets = keep.tile([P, J // 16], U16, name="offsets")
         nc.sync.dma_start(offsets[:], offs)
 
         scale_rows = shared.tile([P, T], U8, name="scale_rows", align_bytes=64, offset=AT_WINDOW)
         nc.gpsimd.memset(scale_rows[:].bitcast(I32), 0)
-        bias = keep.tile([P, N_TILES], F32, name="bias")
-        with nc.allow_non_contiguous_dma(reason="one bias value for each partition"):
-            nc.sync.dma_start(out=bias[:], in_=bg.rearrange("(c p) -> p c", p=P))
-        wg_codes = keep.tile([P, PASSES, 2 * N], U8, name="wg_codes", align_bytes=64)
-        nc.sync.dma_start(out=wg_codes[:].bitcast(I32), in_=wg_words.rearrange("a p b -> p a b").bitcast(I32))
         for r in range(ROWS):
             nc.sync.dma_start(
                 out=scale_rows[r:P:SHIFT, :].bitcast(I32),
                 in_=tab_scales[:, r : QUADS * ROWS : ROWS, :].rearrange("a q t -> q a t").bitcast(I32),
             )
 
-        def load_wh(a):
-            raw = shared.tile([P, PACK, N], F32, name="wh_raw%d" % a, align_bytes=64, offset=AT_RAW[a])
-            rows = wh[a * P * PACK : (a + 1) * P * PACK, :]
-            nc.sync.dma_start(out=raw[:], in_=rows.rearrange("(p i) n -> p i n", i=PACK))
-            return raw
-
-        wh_raw0 = load_wh(0)
-        words = keep.tile([P, T], U32, name="words", align_bytes=64)
-        nc.sync.dma_start(out=words[:].bitcast(I32), in_=tab_words[0].rearrange("p t b -> p (t b)").bitcast(I32))
         wh_raw1 = load_wh(1)
+        words = shared.tile([P, T], U32, name="words", align_bytes=64, offset=AT_WORDS)
+        nc.sync.dma_start(out=words[:].bitcast(I32), in_=tab_words[0].rearrange("p t b -> p (t b)").bitcast(I32))
 
+        wg_codes = keep.tile([P, PASSES, 2 * N], U8, name="wg_codes", align_bytes=64)
+        nc.sync.dma_start(out=wg_codes[:].bitcast(I32), in_=wg_words.rearrange("a p b -> p a b").bitcast(I32))
         wg_planes = keep.tile([P, PASSES, N], U8, name="wg_planes", align_bytes=64)
         nc.gpsimd.memset(wg_planes[:].bitcast(I32), 0)
         for q in range(QUADS):
@@ -91,9 +86,32 @@ def tile_list_hwayt_hl_relu_kernel(
                 out=wg_planes[QUAD * q : QUAD * q + ROWS, :, :].bitcast(I32),
                 in_=wg_scales[:, ROWS * q : ROWS * (q + 1), :].rearrange("a r n -> r a n").bitcast(I32),
             )
+        bias = keep.tile([P, N_TILES], F32, name="bias")
+        with nc.allow_non_contiguous_dma(reason="one bias value for each partition"):
+            nc.sync.dma_start(out=bias[:], in_=bg.rearrange("(c p) -> p c", p=P))
 
         tab_plane1 = keep.tile([P, J], U8, name="tab_plane1", align_bytes=64)
         nc.vector.memset(tab_plane1[P - QUAD : P, :].bitcast(I32), 0)
+
+        warm = keep.tile([P, N_TILES], F32, name="warm")
+        zeros = keep.tile([P, N_TILES], F32, name="zeros")
+        nc.gpsimd.memset(zeros[:], 0.0)
+        nc.scalar.activation(warm[:], zeros[:], ACT.Sigmoid)
+
+        def weave(woven, rows):
+            nc.scalar.copy(out=woven.rearrange("p (n i) -> p n i", i=PACK), in_=rows[:].rearrange("p i n -> p n i"))
+
+        def quantise(name, woven, codes):
+            plane = keep.tile([P, codes.shape[1]], U8, name=name, align_bytes=64)
+            nc.vector.quantize_mx(out=codes[:].bitcast(FP8X4), scales=plane[:], in_=woven[:])
+            return plane
+
+        hi_rows0 = keep.tile([P, PACK, N], F32, name="hi_rows0", align_bytes=64)
+        nc.vector.tensor_scalar(hi_rows0[:].bitcast(I32), wh_raw0[:].bitcast(I32), WORD_MASK, None, ALU.bitwise_and)
+        lo_rows0 = keep.tile([P, PACK, N], BF16, name="lo_rows0", align_bytes=64)
+        nc.gpsimd.tensor_tensor(lo_rows0[:], wh_raw0[:], hi_rows0[:], ALU.subtract)
+        parts0 = keep.tile([P, 2 * N * PACK], BF16, name="parts0", align_bytes=64)
+        weave(parts0[:, 0 : N * PACK], hi_rows0)
 
         picked_scales = keep.tile([P, J], U8, name="picked_scales", align_bytes=64)
         nc.vector.tensor_copy(picked_scales[:], scale_rows[:].indirect(offsets[:]))
@@ -105,25 +123,20 @@ def tile_list_hwayt_hl_relu_kernel(
         r_rows1 = shared.tile([P, T], F32, name="r_rows1", align_bytes=64, offset=AT_R1)
         nc.sync.dma_start(out=r_rows1[:], in_=rT[P : 2 * P, :])
 
-        def weave(a, raw):
-            woven = shared.tile([P, N * PACK], F32, name="woven%d" % a, align_bytes=64, offset=AT_WOVEN[a])
-            nc.scalar.copy(out=woven[:].rearrange("p (n i) -> p n i", i=PACK), in_=raw[:].rearrange("p i n -> p n i"))
-            return woven
-
-
-        woven0 = weave(0, wh_raw0)
-        hi0 = keep.tile([P, N * PACK], F32, name="hi0", align_bytes=64)
-        word_mask = shared.tile([P, 1], I32, name="word_mask", align_bytes=64, offset=AT_PICKED_WORDS)
-        nc.gpsimd.memset(word_mask[:], WORD_MASK)
-        nc.vector.tensor_scalar(hi0[:].bitcast(I32), woven0[:].bitcast(I32), word_mask[:], None, ALU.bitwise_and)
-        parts0 = shared.tile([P, 2, N * PACK], BF16, name="parts0", align_bytes=64, offset=AT_PARTS)
-        nc.gpsimd.tensor_tensor(parts0[:, 1, :], woven0[:], hi0[:], ALU.subtract)
-        nc.scalar.copy(out=parts0[:, 0, :], in_=hi0[:])
+        upper1 = keep.tile([P, PACK, N], BF16, name="upper1", align_bytes=64)
+        nc.scalar.copy(out=upper1[:], in_=wh_raw1[:].bitcast(BF16).rearrange("p i (n e) -> p i n e", e=2)[:, :, :, 1])
+        hi_rows1 = keep.tile([P, PACK, N], BF16, name="hi_rows1", align_bytes=64, tag="hi_rows1")
+        nc.vector.tensor_scalar(hi_rows1[:].bitcast(I32), upper1[:].bitcast(I32), PAIR_MASK, None, ALU.bitwise_and)
+        lo_rows1 = shared.tile([P, PACK, N], BF16, name="lo_rows1", align_bytes=64, offset=AT_PICKED0)
+        nc.gpsimd.tensor_tensor(lo_rows1[:], wh_raw1[:], hi_rows1[:], ALU.subtract)
+        weave(parts0[:, N * PACK : 2 * N * PACK], lo_rows0)
+        parts1 = keep.tile([P, 2 * N * PACK], BF16, name="parts1", align_bytes=64)
+        weave(parts1[:, 0 : N * PACK], hi_rows1)
+        weave(parts1[:, N * PACK : 2 * N * PACK], lo_rows1)
 
         picked_words = shared.tile([P, J], U32, name="picked_words", align_bytes=64, offset=AT_PICKED_WORDS)
         for jt in range(J_TILES):
-            entries = offsets[:, jt * J_TILE // 16 : (jt + 1) * J_TILE // 16]
-            nc.vector.tensor_copy(picked_words[:, columns(jt)], words[:].indirect(entries))
+            nc.vector.tensor_copy(picked_words[:, columns(jt)], words[:].indirect(entries(jt)))
         tab_codes = []
         for jt in range(J_TILES):
             codes = keep.tile([P, PASSES, 2 * J_TILE], U8, name="tab_codes%d" % jt, align_bytes=64)
@@ -132,34 +145,18 @@ def tile_list_hwayt_hl_relu_kernel(
                 picked_words[:, columns(jt)].bitcast(U16).rearrange("p (j a) -> p a j", a=PASSES),
             )
             tab_codes.append(codes)
-        wh_codes0 = keep.tile([P, 2 * N], U32, name="wh_codes0", align_bytes=64)
-        wh_plane0 = keep.tile([P, 2 * N], U8, name="wh_plane0", align_bytes=64)
-        nc.vector.quantize_mx(
-            out=wh_codes0[:].bitcast(FP8X4), scales=wh_plane0[:], in_=parts0[:].rearrange("p h x -> p (h x)")
-        )
 
-        upper1 = keep.tile([P, N, PACK], BF16, name="upper1", align_bytes=64)
-        halves = wh_raw1[:].bitcast(BF16).rearrange("p i (n e) -> p n i e", e=2)
-        nc.scalar.copy(out=upper1[:], in_=halves[:, :, :, 1])
-        woven1 = weave(1, wh_raw1)
-        hi1 = keep.tile([P, N * PACK], BF16, name="hi1", align_bytes=64)
-        nc.vector.tensor_scalar(
-            hi1[:].bitcast(I32), upper1[:].rearrange("p n i -> p (n i)").bitcast(I32), PAIR_MASK, None, ALU.bitwise_and
-        )
-        lo1 = shared.tile([P, N * PACK], BF16, name="lo1", align_bytes=64, offset=AT_PARTS)
-        nc.gpsimd.tensor_tensor(lo1[:], woven1[:], hi1[:], ALU.subtract)
+        wh_passes = []
+        for a, parts in enumerate([parts0, parts1]):
+            codes = shared.tile([P, 2 * N], U32, name="wh_codes%d" % a, align_bytes=64, offset=AT_WORDS + 2 * KB * a)
+            wh_passes.append((codes, quantise("wh_plane%d" % a, parts, codes)))
 
         r_picked0 = shared.tile([P, J], F32, name="r_picked0", align_bytes=64, offset=AT_PICKED0)
-        nc.vector.tensor_copy(r_picked0[:], r_rows0[:].indirect(offsets[:]))
-        hi_codes1 = shared.tile([P, N], U32, name="hi_codes1", align_bytes=64, offset=AT_R0)
-        lo_codes1 = shared.tile([P, N], U32, name="lo_codes1", align_bytes=64, offset=AT_R0 + KB)
-        wh_plane1 = keep.tile([P, 2 * N], U8, name="wh_plane1", align_bytes=64)
-        nc.vector.quantize_mx(out=hi_codes1[:].bitcast(FP8X4), scales=wh_plane1[:, 0:N], in_=hi1[:])
-        nc.vector.quantize_mx(out=lo_codes1[:].bitcast(FP8X4), scales=wh_plane1[:, N : 2 * N], in_=lo1[:])
-        r_picked1 = shared.tile([P, J], F32, name="r_picked1", align_bytes=64, offset=AT_WOVEN[1])
-        nc.vector.tensor_copy(r_picked1[:], r_rows1[:].indirect(offsets[:]))
-        wh_codes = [[wh_codes0[:, 0:N], wh_codes0[:, N : 2 * N]], [hi_codes1[:], lo_codes1[:]]]
-        wh_planes = [wh_plane0, wh_plane1]
+        r_picked1 = keep.tile([P, J], F32, name="r_picked1", align_bytes=64, tag="r_picked1")
+        r_picked = [r_picked0, r_picked1]
+        for c, r_rows in enumerate([r_rows0, r_rows1]):
+            for jt in range(J_TILES):
+                nc.vector.tensor_copy(r_picked[c][:, columns(jt)], r_rows[:].indirect(entries(jt)))
 
         def multiply(acc, weights, weight_plane, a, jt, start, stop):
             nc.tensor.matmul_mx(
@@ -172,55 +169,49 @@ def tile_list_hwayt_hl_relu_kernel(
                 stop=stop,
             )
 
-        half_bias = keep.tile([P, N_TILES], F32, name="half_bias")
-        nc.scalar.activation(half_bias[:], bias[:], ACT.Copy, scale=0.5)
-        losses = []
+        minus_bias = keep.tile([P, N_TILES], F32, name="minus_bias", align_bytes=64, tag="hi_rows1")
+        nc.scalar.activation(minus_bias[:], bias[:], ACT.Copy, scale=-1.0)
+        blocks = [(c, jt) for c in range(N_TILES) for jt in range(J_TILES)]
+        carry = keep.tile([P, N_TILES, J], F32, name="carry", align_bytes=64)
+        for c, jt in blocks:
+            ga = psum.tile([P, J_TILE], F32, name="ga%d%d" % (c, jt), tag="bank%d%d" % (c, jt))
+            for a in reversed(range(PASSES)):
+                weights = wg_codes[:, a, 2 * c * P : 2 * (c + 1) * P].bitcast(FP4X4)
+                multiply(ga, weights, wg_planes[:, a, c * P : (c + 1) * P], a, jt, a == PASSES - 1, a == 0)
+            nc.scalar.activation(
+                carry[:, c, columns(jt)], ga[:], ACT.Sigmoid, bias=minus_bias[:, c : c + 1], scale=-1.0
+            )
+        gates = []
         for c in range(N_TILES):
-            tanh = keep.tile([P, J], F32, name="tanh%d" % c, align_bytes=64)
-            loss = keep.tile([P, J], F32, name="loss%d" % c, align_bytes=64, tag="loss%d" % c)
-            for jt in range(J_TILES):
-                ga = psum.tile([P, J_TILE], F32, name="ga%d%d" % (c, jt), tag="bank%d%d" % (c, jt))
-                for a in reversed(range(PASSES)):
-                    weights = wg_codes[:, a, 2 * c * P : 2 * (c + 1) * P].bitcast(FP4X4)
-                    multiply(ga, weights, wg_planes[:, a, c * P : (c + 1) * P], a, jt, a == PASSES - 1, a == 0)
-                nc.scalar.activation(
-                    tanh[:, columns(jt)], ga[:], ACT.Tanh, bias=half_bias[:, c : c + 1], scale=0.5
-                )
-                nc.scalar.activation(loss[:, columns(jt)], tanh[:, columns(jt)], ACT.Copy, bias=-0.5, scale=0.5)
-            losses.append(loss)
+            gate = keep.tile([P, J], F32, name="gate%d" % c, align_bytes=64)
+            nc.scalar.activation(gate[:], carry[:, c, :], ACT.Copy, bias=1.0, scale=-1.0)
+            gates.append(gate)
 
         ha = {}
-        for c in range(N_TILES):
-            for jt in range(J_TILES):
-                ha[c, jt] = psum.tile([P, J_TILE], F32, name="ha%d%d" % (c, jt), tag="bank%d%d" % (c, jt))
-            for a in range(PASSES):
-                for jt in range(J_TILES):
-                    for part in range(2):
-                        codes = wh_codes[a][part][:, c * P : (c + 1) * P].bitcast(FP8X4)
-                        plane = wh_planes[a][:, part * N + c * P : part * N + (c + 1) * P]
-                        start, stop = (a, part) == (0, 0), (a, part) == (PASSES - 1, 1)
-                        multiply(ha[c, jt], codes, plane, a, jt, start, stop)
+        for c, jt in blocks:
+            ha[c, jt] = psum.tile([P, J_TILE], F32, name="ha%d%d" % (c, jt), tag="bank%d%d" % (c, jt))
+            for a, (codes, plane) in enumerate(wh_passes):
+                for part in range(2):
+                    own = slice(part * N + c * P, part * N + (c + 1) * P)
+                    start, stop = (a, part) == (0, 0), (a, part) == (PASSES - 1, 1)
+                    multiply(ha[c, jt], codes[:, own].bitcast(FP8X4), plane[:, own], a, jt, start, stop)
 
-        lost0 = shared.tile([P, J], F32, name="lost0", align_bytes=64, offset=AT_PARTS)
-        nc.gpsimd.tensor_tensor(lost0[:], r_picked0[:], losses[0][:], ALU.mult)
-        lost1 = keep.tile([P, J], F32, name="lost1", align_bytes=64)
-        nc.gpsimd.tensor_tensor(lost1[:], r_picked1[:], losses[1][:], ALU.mult)
+        kept = keep.tile([P, N_TILES, J], F32, name="kept", align_bytes=64)
+        for c, jt in blocks:
+            nc.gpsimd.tensor_tensor(
+                kept[:, c, columns(jt)], r_picked[c][:, columns(jt)], carry[:, c, columns(jt)], ALU.mult
+            )
 
         made = shared.tile([P, N_TILES, J], F32, name="made", align_bytes=64, offset=AT_R1)
-        for c in range(N_TILES):
-            for jt in range(J_TILES):
-                nc.vector.scalar_tensor_tensor(
-                    made[:, c, columns(jt)], losses[c][:, columns(jt)], 1.0, ha[c, jt][:], ALU.add, ALU.mult
-                )
-
-        result0 = keep.tile([P, J], F32, name="result0", align_bytes=64, tag="loss1")
-        for jt in range(J_TILES):
+        for c, jt in blocks:
             nc.vector.scalar_tensor_tensor(
-                result0[:, columns(jt)], made[:, 0, columns(jt)], 0.0, lost0[:, columns(jt)], ALU.max, ALU.subtract
+                made[:, c, columns(jt)], ha[c, jt][:], 0.0, gates[c][:, columns(jt)], ALU.max, ALU.mult
             )
-            nc.sync.dma_start(out=out[0:P, columns(jt)], in_=result0[:, columns(jt)])
-        edges = [0, J_TILE, J_TILE + J_TILE // 2, J]
-        for lo, hi in zip(edges, edges[1:]):
-            result1 = keep.tile([P, hi - lo], F32, name="result1_%d" % lo, align_bytes=64)
-            nc.vector.scalar_tensor_tensor(result1[:], made[:, 1, lo:hi], 0.0, lost1[:, lo:hi], ALU.max, ALU.subtract)
-            nc.sync.dma_start(out=out[P : 2 * P, lo:hi], in_=result1[:])
+
+        result0 = keep.tile([P, J], F32, name="result0", align_bytes=64, tag="r_picked1")
+        result1 = keep.tile([P, J], F32, name="result1", align_bytes=64)
+        for c, result in enumerate([result0, result1]):
+            for lo in range(0, J, STORE):
+                piece = slice(lo, lo + STORE)
+                nc.vector.tensor_tensor(result[:, piece], made[:, c, piece], kept[:, c, piece], ALU.add)
+                nc.sync.dma_start(out=out[c * P : (c + 1) * P, piece], in_=result[:, piece])

@@ -25,6 +25,7 @@ J_TILES = J // J_TILE
 QUAD = 32
 QUADS = P // QUAD
 ROWS = 4
+R_PIECES = (((0, 256), (256, 512), (512, 1024)), ((0, 512), (512, 1024)))
 STORE = 256
 SHIFT = 16
 WORD_MASK = 0xFFF00000 - (1 << 32)
@@ -155,8 +156,8 @@ def tile_list_hwayt_hl_relu_kernel(
         r_picked1 = keep.tile([P, J], F32, name="r_picked1", align_bytes=64, tag="r_picked1")
         r_picked = [r_picked0, r_picked1]
         for c, r_rows in enumerate([r_rows0, r_rows1]):
-            for jt in range(J_TILES):
-                nc.vector.tensor_copy(r_picked[c][:, columns(jt)], r_rows[:].indirect(entries(jt)))
+            for lo, hi in R_PIECES[c]:
+                nc.vector.tensor_copy(r_picked[c][:, lo:hi], r_rows[:].indirect(offsets[:, lo // 16 : hi // 16]))
 
         def multiply(acc, weights, weight_plane, a, jt, start, stop):
             nc.tensor.matmul_mx(
@@ -197,10 +198,9 @@ def tile_list_hwayt_hl_relu_kernel(
                     multiply(ha[c, jt], codes[:, own].bitcast(FP8X4), plane[:, own], a, jt, start, stop)
 
         kept = keep.tile([P, N_TILES, J], F32, name="kept", align_bytes=64)
-        for c, jt in blocks:
-            nc.gpsimd.tensor_tensor(
-                kept[:, c, columns(jt)], r_picked[c][:, columns(jt)], carry[:, c, columns(jt)], ALU.mult
-            )
+        for c in range(N_TILES):
+            for lo, hi in R_PIECES[c]:
+                nc.gpsimd.tensor_tensor(kept[:, c, lo:hi], r_picked[c][:, lo:hi], carry[:, c, lo:hi], ALU.mult)
 
         made = shared.tile([P, N_TILES, J], F32, name="made", align_bytes=64, offset=AT_R1)
         for c, jt in blocks:
@@ -210,8 +210,11 @@ def tile_list_hwayt_hl_relu_kernel(
 
         result0 = keep.tile([P, J], F32, name="result0", align_bytes=64, tag="r_picked1")
         result1 = keep.tile([P, J], F32, name="result1", align_bytes=64)
+        first = keep.tile([P, STORE], F32, name="first", align_bytes=64)
+        nc.gpsimd.tensor_tensor(first[:], made[:, 0, 0:STORE], kept[:, 0, 0:STORE], ALU.add)
+        nc.sync.dma_start(out=out[0:P, 0:STORE], in_=first[:])
         for c, result in enumerate([result0, result1]):
-            for lo in range(0, J, STORE):
+            for lo in range(STORE if c == 0 else 0, J, STORE):
                 piece = slice(lo, lo + STORE)
                 nc.vector.tensor_tensor(result[:, piece], made[:, c, piece], kept[:, c, piece], ALU.add)
                 nc.sync.dma_start(out=out[c * P : (c + 1) * P, piece], in_=result[:, piece])

@@ -25,7 +25,7 @@ J_TILES = J // J_TILE
 QUAD = 32
 QUADS = P // QUAD
 ROWS = 4
-R_PIECES = (((0, 256), (256, 512), (512, 1024)), ((0, 512), (512, 1024)))
+R_PIECES = (((0, 256), (256, 576), (576, 1024)), ((0, 512), (512, 1024)))
 STORE = 256
 SHIFT = 16
 WORD_MASK = 0xFFF00000 - (1 << 32)
@@ -112,7 +112,10 @@ def tile_list_hwayt_hl_relu_kernel(
         lo_rows0 = keep.tile([P, PACK, N], BF16, name="lo_rows0", align_bytes=64)
         nc.gpsimd.tensor_tensor(lo_rows0[:], wh_raw0[:], hi_rows0[:], ALU.subtract)
         parts0 = keep.tile([P, 2 * N * PACK], BF16, name="parts0", align_bytes=64)
-        weave(parts0[:, 0 : N * PACK], hi_rows0)
+        nc.scalar.copy(
+            out=parts0[:, 0 : N * PACK].rearrange("p (g m i) -> p g i m", m=PACK, i=PACK),
+            in_=hi_rows0[:].rearrange("p i (g m) -> p g i m", m=PACK),
+        )
 
         picked_scales = keep.tile([P, J], U8, name="picked_scales", align_bytes=64)
         nc.vector.tensor_copy(picked_scales[:], scale_rows[:].indirect(offsets[:]))

@@ -56,13 +56,15 @@ def tile_list_hwayt_hl_relu_kernel(
         def entries(jt):
             return offsets[:, jt * J_TILE // 16 : (jt + 1) * J_TILE // 16]
 
-        def load_wh(a):
+        def load_wh(a, pieces):
             raw = keep.tile([P, PACK, N], F32, name="wh_raw%d" % a, align_bytes=64)
-            rows = wh[a * P * PACK : (a + 1) * P * PACK, :]
-            nc.sync.dma_start(out=raw[:], in_=rows.rearrange("(p i) n -> p i n", i=PACK))
+            rows = wh[a * P * PACK : (a + 1) * P * PACK, :].rearrange("(p i) n -> p i n", i=PACK)
+            for piece in pieces:
+                nc.sync.dma_start(out=raw[:, piece, :], in_=rows[:, piece, :])
             return raw
 
-        wh_raw0 = load_wh(0)
+        halves = [slice(0, PACK // 2), slice(PACK // 2, PACK)]
+        wh_raw0 = load_wh(0, halves)
         offsets = keep.tile([P, J // 16], U16, name="offsets")
         nc.sync.dma_start(offsets[:], offs)
 
@@ -74,7 +76,7 @@ def tile_list_hwayt_hl_relu_kernel(
                 in_=tab_scales[:, r : QUADS * ROWS : ROWS, :].rearrange("a q t -> q a t").bitcast(I32),
             )
 
-        wh_raw1 = load_wh(1)
+        wh_raw1 = load_wh(1, [slice(0, PACK)])
         words = shared.tile([P, T], U32, name="words", align_bytes=64, offset=AT_WORDS)
         nc.sync.dma_start(out=words[:].bitcast(I32), in_=tab_words[0].rearrange("p t b -> p (t b)").bitcast(I32))
 
@@ -108,7 +110,10 @@ def tile_list_hwayt_hl_relu_kernel(
             return plane
 
         hi_rows0 = keep.tile([P, PACK, N], F32, name="hi_rows0", align_bytes=64)
-        nc.vector.tensor_scalar(hi_rows0[:].bitcast(I32), wh_raw0[:].bitcast(I32), WORD_MASK, None, ALU.bitwise_and)
+        for half in halves:
+            nc.vector.tensor_scalar(
+                hi_rows0[:, half, :].bitcast(I32), wh_raw0[:, half, :].bitcast(I32), WORD_MASK, None, ALU.bitwise_and
+            )
         lo_rows0 = keep.tile([P, PACK, N], BF16, name="lo_rows0", align_bytes=64)
         nc.gpsimd.tensor_tensor(lo_rows0[:], wh_raw0[:], hi_rows0[:], ALU.subtract)
         parts0 = keep.tile([P, 2 * N * PACK], BF16, name="parts0", align_bytes=64)

@@ -222,7 +222,8 @@ def tile_list_hwayt_hl_relu_kernel(
         nc.gpsimd.tensor_tensor(first[:], made[:, 0, 0:STORE], kept[:, 0, 0:STORE], ALU.add)
         nc.sync.dma_start(out=out[0:P, 0:STORE], in_=first[:])
         for c, result in enumerate([result0, result1]):
-            for lo in range(STORE if c == 0 else 0, J, STORE):
-                piece = slice(lo, lo + STORE)
+            edges = list(range(STORE, J + 1, STORE)) if c == 0 else list(range(0, J, STORE)) + [J - STORE // 2, J]
+            for lo, hi in zip(edges, edges[1:]):
+                piece = slice(lo, hi)
                 nc.vector.tensor_tensor(result[:, piece], made[:, c, piece], kept[:, c, piece], ALU.add)
                 nc.sync.dma_start(out=out[c * P : (c + 1) * P, piece], in_=result[:, piece])

@@ -22,22 +22,27 @@ PASSES = K // (P * PACK)
 N_TILES = N // P
 J_TILE = 512
 J_TILES = J // J_TILE
+QUARTER = J // 4
 QUAD = 32
 QUADS = P // QUAD
 ROWS = 4
-R_PIECES = (((0, 256), (256, 576), (576, 1024)), ((0, 512), (512, 1024)))
 STORE = 256
 SHIFT = 16
 WORD_MASK = 0xFFF00000 - (1 << 32)
 PAIR_MASK = 0xFFF0FFF0 - (1 << 32)
+PART = N * PACK
 
 KB = 1024
-AT_WINDOW = 8 * KB
-AT_R1 = KB // 2
-AT_R0 = 9 * KB + KB // 2
-AT_WORDS = 18 * KB
-AT_PICKED_WORDS = 26 * KB
-AT_PICKED0 = 30 * KB
+AT_R1 = 0
+AT_WINDOW = 8 * KB - 256
+AT_RAW0 = 50 * KB
+AT_R0 = 10 * KB - 512
+AT_GATES = 18 * KB
+AT_WOVEN_LO = 25 * KB + 512
+AT_WOVEN_HI0 = 29 * KB
+AT_PICKED = 30 * KB
+AT_MADE = 35 * KB
+AT_RESULT = 43 * KB
 
 
 def columns(jt):
@@ -53,18 +58,17 @@ def tile_list_hwayt_hl_relu_kernel(
         shared = ctx.enter_context(tc.tile_pool(name="shared", bufs=1))
         psum = ctx.enter_context(tc.psum_pool(name="psum", bufs=1))
 
-        def entries(jt):
-            return offsets[:, jt * J_TILE // 16 : (jt + 1) * J_TILE // 16]
+        def entries(lo, hi):
+            return offsets[:, lo // 16 : hi // 16]
 
-        def load_wh(a, pieces):
-            raw = keep.tile([P, PACK, N], F32, name="wh_raw%d" % a, align_bytes=64)
+        def load_wh(a, raw, pieces):
             rows = wh[a * P * PACK : (a + 1) * P * PACK, :].rearrange("(p i) n -> p i n", i=PACK)
             for piece in pieces:
                 nc.sync.dma_start(out=raw[:, piece, :], in_=rows[:, piece, :])
-            return raw
 
         halves = [slice(0, PACK // 2), slice(PACK // 2, PACK)]
-        wh_raw0 = load_wh(0, halves)
+        wh_raw0 = shared.tile([P, PACK, N], F32, name="wh_raw0", align_bytes=64, offset=AT_RAW0)
+        load_wh(0, wh_raw0, halves)
         offsets = keep.tile([P, J // 16], U16, name="offsets")
         nc.sync.dma_start(offsets[:], offs)
 
@@ -75,9 +79,9 @@ def tile_list_hwayt_hl_relu_kernel(
                 out=scale_rows[r:P:SHIFT, :].bitcast(I32),
                 in_=tab_scales[:, r : QUADS * ROWS : ROWS, :].rearrange("a q t -> q a t").bitcast(I32),
             )
-
-        wh_raw1 = load_wh(1, [slice(0, PACK)])
-        words = shared.tile([P, T], U32, name="words", align_bytes=64, offset=AT_WORDS)
+        wh_raw1 = keep.tile([P, PACK, N], F32, name="wh_raw1", align_bytes=64)
+        load_wh(1, wh_raw1, [slice(0, PACK)])
+        words = keep.tile([P, T], U32, name="words", align_bytes=64)
         nc.sync.dma_start(out=words[:].bitcast(I32), in_=tab_words[0].rearrange("p t b -> p (t b)").bitcast(I32))
 
         wg_codes = keep.tile([P, PASSES, 2 * N], U8, name="wg_codes", align_bytes=64)
@@ -101,26 +105,33 @@ def tile_list_hwayt_hl_relu_kernel(
         nc.gpsimd.memset(zeros[:], 0.0)
         nc.scalar.activation(warm[:], zeros[:], ACT.Sigmoid)
 
-        def weave(woven, rows):
-            nc.scalar.copy(out=woven.rearrange("p (n i) -> p n i", i=PACK), in_=rows[:].rearrange("p i n -> p n i"))
+        def own(c):
+            return slice(c * P, (c + 1) * P)
+
+        def weave_hi(woven, rows):
+            nc.scalar.copy(
+                out=woven.rearrange("p (g m i) -> p g i m", m=PACK, i=PACK),
+                in_=rows.rearrange("p i (g m) -> p g i m", m=PACK),
+            )
+
+        def weave_lo(woven, rows):
+            nc.scalar.copy(out=woven.rearrange("p (n i) -> p n i", i=PACK), in_=rows.rearrange("p i n -> p n i"))
 
         def quantise(name, woven, codes):
-            plane = keep.tile([P, codes.shape[1]], U8, name=name, align_bytes=64)
+            width = codes.shape[1]
+            plane = keep.tile([P, width], U8, name="plane" + name, align_bytes=64)
             nc.vector.quantize_mx(out=codes[:].bitcast(FP8X4), scales=plane[:], in_=woven[:])
-            return plane
+            return codes, plane
 
         hi_rows0 = keep.tile([P, PACK, N], F32, name="hi_rows0", align_bytes=64)
         for half in halves:
             nc.vector.tensor_scalar(
                 hi_rows0[:, half, :].bitcast(I32), wh_raw0[:, half, :].bitcast(I32), WORD_MASK, None, ALU.bitwise_and
             )
-        lo_rows0 = keep.tile([P, PACK, N], BF16, name="lo_rows0", align_bytes=64)
+        lo_rows0 = keep.tile([P, PACK, N], BF16, name="lo_rows0", align_bytes=64, tag="lo_rows0")
         nc.gpsimd.tensor_tensor(lo_rows0[:], wh_raw0[:], hi_rows0[:], ALU.subtract)
-        parts0 = keep.tile([P, 2 * N * PACK], BF16, name="parts0", align_bytes=64)
-        nc.scalar.copy(
-            out=parts0[:, 0 : N * PACK].rearrange("p (g m i) -> p g i m", m=PACK, i=PACK),
-            in_=hi_rows0[:].rearrange("p i (g m) -> p g i m", m=PACK),
-        )
+        woven_hi0 = shared.tile([P, PART], BF16, name="woven_hi0", align_bytes=64, offset=AT_WOVEN_HI0)
+        weave_hi(woven_hi0[:], hi_rows0[:])
 
         picked_scales = keep.tile([P, J], U8, name="picked_scales", align_bytes=64)
         nc.vector.tensor_copy(picked_scales[:], scale_rows[:].indirect(offsets[:]))
@@ -131,99 +142,113 @@ def tile_list_hwayt_hl_relu_kernel(
         nc.sync.dma_start(out=r_rows0[:], in_=rT[0:P, :])
         r_rows1 = shared.tile([P, T], F32, name="r_rows1", align_bytes=64, offset=AT_R1)
         nc.sync.dma_start(out=r_rows1[:], in_=rT[P : 2 * P, :])
+        r_rows = [r_rows0, r_rows1]
 
-        upper1 = keep.tile([P, PACK, N], BF16, name="upper1", align_bytes=64)
-        nc.scalar.copy(out=upper1[:], in_=wh_raw1[:].bitcast(BF16).rearrange("p i (n e) -> p i n e", e=2)[:, :, :, 1])
-        hi_rows1 = keep.tile([P, PACK, N], BF16, name="hi_rows1", align_bytes=64, tag="hi_rows1")
-        nc.vector.tensor_scalar(hi_rows1[:].bitcast(I32), upper1[:].bitcast(I32), PAIR_MASK, None, ALU.bitwise_and)
-        lo_rows1 = shared.tile([P, PACK, N], BF16, name="lo_rows1", align_bytes=64, offset=AT_PICKED0)
-        nc.gpsimd.tensor_tensor(lo_rows1[:], wh_raw1[:], hi_rows1[:], ALU.subtract)
-        weave(parts0[:, N * PACK : 2 * N * PACK], lo_rows0)
-        parts1 = keep.tile([P, 2 * N * PACK], BF16, name="parts1", align_bytes=64)
-        weave(parts1[:, 0 : N * PACK], hi_rows1)
-        weave(parts1[:, N * PACK : 2 * N * PACK], lo_rows1)
+        upper1 = keep.tile([P, PART], BF16, name="upper1", align_bytes=64)
+        weave_hi(upper1[:], wh_raw1[:].bitcast(BF16).rearrange("p i (n e) -> p i n e", e=2)[:, :, :, 1])
+        woven_hi1 = keep.tile([P, PART], BF16, name="woven_hi1", align_bytes=64)
+        nc.vector.tensor_scalar(woven_hi1[:].bitcast(I32), upper1[:].bitcast(I32), PAIR_MASK, None, ALU.bitwise_and)
+        codes_hi0 = shared.tile([P, N], U32, name="codes_hi0", align_bytes=64, offset=AT_RAW0)
+        codes_hi1 = shared.tile([P, N], U32, name="codes_hi1", align_bytes=64, offset=AT_RAW0 + KB)
+        hi_parts = [quantise("hi0", woven_hi0, codes_hi0), quantise("hi1", woven_hi1, codes_hi1)]
+        woven_lo = shared.tile([P, PASSES * PART], BF16, name="woven_lo", align_bytes=64, offset=AT_WOVEN_LO)
+        weave_lo(woven_lo[:, 0:PART], lo_rows0[:])
+        nc.gpsimd.tensor_tensor(
+            woven_lo[:, PART : 2 * PART].rearrange("p (n i) -> p n i", i=PACK),
+            wh_raw1[:].rearrange("p i n -> p n i"),
+            woven_hi1[:].rearrange("p (n i) -> p n i", i=PACK),
+            ALU.subtract,
+        )
+        minus_bias = keep.tile([P, N_TILES], F32, name="minus_bias", align_bytes=64, tag="lo_rows0")
+        nc.scalar.activation(minus_bias[:], bias[:], ACT.Copy, scale=-1.0)
 
-        picked_words = shared.tile([P, J], U32, name="picked_words", align_bytes=64, offset=AT_PICKED_WORDS)
+        picked_words = shared.tile([P, J], U32, name="picked_words", align_bytes=64, offset=AT_PICKED)
         for jt in range(J_TILES):
-            nc.vector.tensor_copy(picked_words[:, columns(jt)], words[:].indirect(entries(jt)))
-        tab_codes = []
-        for jt in range(J_TILES):
-            codes = keep.tile([P, PASSES, 2 * J_TILE], U8, name="tab_codes%d" % jt, align_bytes=64)
+            nc.vector.tensor_copy(picked_words[:, columns(jt)], words[:].indirect(entries(jt * J_TILE, (jt + 1) * J_TILE)))
+        tab_codes = [keep.tile([P, PASSES, J_TILE], U16, name="tab_codes%d" % jt, align_bytes=64) for jt in range(J_TILES)]
+        for lo, hi in ((0, QUARTER), (QUARTER, J_TILE), (J_TILE, J)):
             nc.vector.tensor_copy(
-                codes[:].bitcast(U16),
-                picked_words[:, columns(jt)].bitcast(U16).rearrange("p (j a) -> p a j", a=PASSES),
+                tab_codes[lo // J_TILE][:, :, lo % J_TILE : lo % J_TILE + hi - lo],
+                picked_words[:, lo:hi].bitcast(U16).rearrange("p (j a) -> p a j", a=PASSES),
             )
-            tab_codes.append(codes)
+        codes_lo = keep.tile([P, PASSES * N], U32, name="codes_lo", align_bytes=64)
+        plane_lo = quantise("lo", woven_lo, codes_lo)[1]
 
-        wh_passes = []
-        for a, parts in enumerate([parts0, parts1]):
-            codes = shared.tile([P, 2 * N], U32, name="wh_codes%d" % a, align_bytes=64, offset=AT_WORDS + 2 * KB * a)
-            wh_passes.append((codes, quantise("wh_plane%d" % a, parts, codes)))
-
-        r_picked0 = shared.tile([P, J], F32, name="r_picked0", align_bytes=64, offset=AT_PICKED0)
-        r_picked1 = keep.tile([P, J], F32, name="r_picked1", align_bytes=64, tag="r_picked1")
-        r_picked = [r_picked0, r_picked1]
-        for c, r_rows in enumerate([r_rows0, r_rows1]):
-            for lo, hi in R_PIECES[c]:
-                nc.vector.tensor_copy(r_picked[c][:, lo:hi], r_rows[:].indirect(offsets[:, lo // 16 : hi // 16]))
-
-        def multiply(acc, weights, weight_plane, a, jt, start, stop):
+        def multiply(acc, weights, weight_plane, a, jt, cols, start, stop):
             nc.tensor.matmul_mx(
-                out=acc[:],
+                out=acc[:, cols],
                 lhsT=weights,
                 lhsT_scale=weight_plane,
-                rhs=tab_codes[jt][:, a, :].bitcast(FP4X4),
-                rhs_scale=tab_planes[a][:, columns(jt)],
+                rhs=tab_codes[jt][:, a, cols].bitcast(U8).bitcast(FP4X4),
+                rhs_scale=tab_planes[a][:, columns(jt)][:, cols],
                 start=start,
                 stop=stop,
             )
 
-        minus_bias = keep.tile([P, N_TILES], F32, name="minus_bias", align_bytes=64, tag="hi_rows1")
-        nc.scalar.activation(minus_bias[:], bias[:], ACT.Copy, scale=-1.0)
+        whole, left, right = slice(0, J_TILE), slice(0, QUARTER), slice(QUARTER, J_TILE)
         blocks = [(c, jt) for c in range(N_TILES) for jt in range(J_TILES)]
-        carry = keep.tile([P, N_TILES, J], F32, name="carry", align_bytes=64)
+        ha, carry = {}, {}
         for c, jt in blocks:
-            ga = psum.tile([P, J_TILE], F32, name="ga%d%d" % (c, jt), tag="bank%d%d" % (c, jt))
+            if (c, jt) == (1, 0):
+                carry[c, jt] = shared.tile([P, J_TILE], F32, name="carry10", align_bytes=64, offset=AT_MADE)
+            else:
+                carry[c, jt] = keep.tile([P, J_TILE], F32, name="carry%d%d" % (c, jt), align_bytes=64)
+
+        def gate_passes(acc, c, jt, cols):
             for a in reversed(range(PASSES)):
                 weights = wg_codes[:, a, 2 * c * P : 2 * (c + 1) * P].bitcast(FP4X4)
-                multiply(ga, weights, wg_planes[:, a, c * P : (c + 1) * P], a, jt, a == PASSES - 1, a == 0)
+                multiply(acc, weights, wg_planes[:, a, own(c)], a, jt, cols, a == PASSES - 1, a == 0)
+
+        def sigmoid(acc, c, jt, cols):
             nc.scalar.activation(
-                carry[:, c, columns(jt)], ga[:], ACT.Sigmoid, bias=minus_bias[:, c : c + 1], scale=-1.0
+                carry[c, jt][:, cols], acc[:, cols], ACT.Sigmoid, bias=minus_bias[:, c : c + 1], scale=-1.0
             )
-        gates = []
-        for c in range(N_TILES):
-            gate = keep.tile([P, J], F32, name="gate%d" % c, align_bytes=64)
-            nc.scalar.activation(gate[:], carry[:, c, :], ACT.Copy, bias=1.0, scale=-1.0)
-            gates.append(gate)
 
-        ha = {}
+        def bank(name, tag):
+            return psum.tile([P, J_TILE], F32, name=name, tag=tag)
+
+        for (c, jt, cols), tag in zip(
+            ((0, 0, left), (0, 0, right), (0, 1, left), (0, 1, right), (1, 0, whole), (1, 1, whole)), range(6)
+        ):
+            acc = bank("ga%d" % tag, "bank%d" % tag)
+            gate_passes(acc, c, jt, cols)
+            sigmoid(acc, c, jt, cols)
+        for (c, jt), tag in zip(blocks, range(4)):
+            ha[c, jt] = bank("ha%d%d" % (c, jt), "bank%d" % tag)
+            for a in range(PASSES):
+                codes, plane = hi_parts[a]
+                multiply(ha[c, jt], codes[:, own(c)].bitcast(FP8X4), plane[:, own(c)], a, jt, whole, a == 0, False)
+            for a in range(PASSES):
+                cols = slice(a * N + c * P, a * N + (c + 1) * P)
+                multiply(ha[c, jt], codes_lo[:, cols].bitcast(FP8X4), plane_lo[:, cols], a, jt, whole, False, a == PASSES - 1)
+
+        kept = {}
         for c, jt in blocks:
-            ha[c, jt] = psum.tile([P, J_TILE], F32, name="ha%d%d" % (c, jt), tag="bank%d%d" % (c, jt))
-            for a, (codes, plane) in enumerate(wh_passes):
-                for part in range(2):
-                    own = slice(part * N + c * P, part * N + (c + 1) * P)
-                    start, stop = (a, part) == (0, 0), (a, part) == (PASSES - 1, 1)
-                    multiply(ha[c, jt], codes[:, own].bitcast(FP8X4), plane[:, own], a, jt, start, stop)
+            if (c, jt) == (0, 0):
+                kept[c, jt] = shared.tile([P, J_TILE], F32, name="kept00", align_bytes=64, offset=AT_RESULT)
+            else:
+                kept[c, jt] = keep.tile([P, J_TILE], F32, name="kept%d%d" % (c, jt), align_bytes=64)
+            for cols in (left, right) if c == 0 else (whole,):
+                window = r_rows[c][:].indirect(entries(jt * J_TILE + cols.start, jt * J_TILE + cols.stop))
+                nc.vector.tensor_tensor(kept[c, jt][:, cols], window, carry[c, jt][:, cols], ALU.mult)
 
-        kept = keep.tile([P, N_TILES, J], F32, name="kept", align_bytes=64)
-        for c in range(N_TILES):
-            for lo, hi in R_PIECES[c]:
-                nc.gpsimd.tensor_tensor(kept[:, c, lo:hi], r_picked[c][:, lo:hi], carry[:, c, lo:hi], ALU.mult)
-
-        made = shared.tile([P, N_TILES, J], F32, name="made", align_bytes=64, offset=AT_R1)
+        gates = shared.tile([P, N_TILES, J], F32, name="gates", align_bytes=64, offset=AT_R0)
+        made = shared.tile([P, N_TILES, J], F32, name="made", align_bytes=64, offset=AT_MADE)
         for c, jt in blocks:
+            nc.scalar.activation(gates[:, c, columns(jt)], carry[c, jt][:], ACT.Copy, bias=1.0, scale=-1.0)
             nc.vector.scalar_tensor_tensor(
-                made[:, c, columns(jt)], ha[c, jt][:], 0.0, gates[c][:, columns(jt)], ALU.max, ALU.mult
+                made[:, c, columns(jt)], ha[c, jt][:], 0.0, gates[:, c, columns(jt)], ALU.max, ALU.mult
             )
 
-        result0 = keep.tile([P, J], F32, name="result0", align_bytes=64, tag="r_picked1")
-        result1 = keep.tile([P, J], F32, name="result1", align_bytes=64)
-        first = keep.tile([P, STORE], F32, name="first", align_bytes=64)
-        nc.gpsimd.tensor_tensor(first[:], made[:, 0, 0:STORE], kept[:, 0, 0:STORE], ALU.add)
-        nc.sync.dma_start(out=out[0:P, 0:STORE], in_=first[:])
-        for c, result in enumerate([result0, result1]):
-            edges = list(range(STORE, J + 1, STORE)) if c == 0 else list(range(0, J, STORE)) + [J - STORE // 2, J]
+        def add_and_store(engine, result, c, jt, edges):
             for lo, hi in zip(edges, edges[1:]):
-                piece = slice(lo, hi)
-                nc.vector.tensor_tensor(result[:, piece], made[:, c, piece], kept[:, c, piece], ALU.add)
-                nc.sync.dma_start(out=out[c * P : (c + 1) * P, piece], in_=result[:, piece])
+                span = slice(jt * J_TILE + lo, jt * J_TILE + hi)
+                engine.tensor_tensor(result[:, lo:hi], made[:, c, span], kept[c, jt][:, lo:hi], ALU.add)
+                nc.sync.dma_start(out=out[own(c), span], in_=result[:, lo:hi])
+
+        first = keep.tile([P, J_TILE], F32, name="first", align_bytes=64)
+        add_and_store(nc.gpsimd, first[:], 0, 0, (0, J_TILE))
+        result = shared.tile([P, 3, J_TILE], F32, name="result", align_bytes=64, offset=AT_RESULT)
+        add_and_store(nc.vector, result[:, 0, :], 0, 1, (0, STORE, J_TILE))
+        add_and_store(nc.vector, result[:, 1, :], 1, 0, (0, STORE, J_TILE))
+        add_and_store(nc.vector, result[:, 2, :], 1, 1, (0, STORE, J_TILE - STORE // 2, J_TILE))

@@ -37,10 +37,8 @@ AT_R1 = 0
 AT_WINDOW = 8 * KB - 256
 AT_RAW0 = 50 * KB
 AT_R0 = 10 * KB - 512
-AT_GATES = 18 * KB
-AT_WOVEN_LO = 25 * KB + 512
-AT_WOVEN_HI0 = 29 * KB
-AT_PICKED = 30 * KB
+AT_UPPER1 = 29 * KB
+AT_PICKED = 27 * KB + 512
 AT_MADE = 35 * KB
 AT_RESULT = 43 * KB
 
@@ -130,7 +128,7 @@ def tile_list_hwayt_hl_relu_kernel(
             )
         lo_rows0 = keep.tile([P, PACK, N], BF16, name="lo_rows0", align_bytes=64, tag="lo_rows0")
         nc.gpsimd.tensor_tensor(lo_rows0[:], wh_raw0[:], hi_rows0[:], ALU.subtract)
-        woven_hi0 = shared.tile([P, PART], BF16, name="woven_hi0", align_bytes=64, offset=AT_WOVEN_HI0)
+        woven_hi0 = keep.tile([P, PART], BF16, name="woven_hi0", align_bytes=64)
         weave_hi(woven_hi0[:], hi_rows0[:])
 
         picked_scales = keep.tile([P, J], U8, name="picked_scales", align_bytes=64)
@@ -144,14 +142,13 @@ def tile_list_hwayt_hl_relu_kernel(
         nc.sync.dma_start(out=r_rows1[:], in_=rT[P : 2 * P, :])
         r_rows = [r_rows0, r_rows1]
 
-        upper1 = keep.tile([P, PART], BF16, name="upper1", align_bytes=64)
+        upper1 = shared.tile([P, PART], BF16, name="upper1", align_bytes=64, offset=AT_UPPER1)
         weave_hi(upper1[:], wh_raw1[:].bitcast(BF16).rearrange("p i (n e) -> p i n e", e=2)[:, :, :, 1])
-        woven_hi1 = keep.tile([P, PART], BF16, name="woven_hi1", align_bytes=64)
+        woven_hi1 = shared.tile([P, PART], BF16, name="woven_hi1", align_bytes=64, offset=AT_RAW0 + KB)
         nc.vector.tensor_scalar(woven_hi1[:].bitcast(I32), upper1[:].bitcast(I32), PAIR_MASK, None, ALU.bitwise_and)
         codes_hi0 = shared.tile([P, N], U32, name="codes_hi0", align_bytes=64, offset=AT_RAW0)
-        codes_hi1 = shared.tile([P, N], U32, name="codes_hi1", align_bytes=64, offset=AT_RAW0 + KB)
-        hi_parts = [quantise("hi0", woven_hi0, codes_hi0), quantise("hi1", woven_hi1, codes_hi1)]
-        woven_lo = shared.tile([P, PASSES * PART], BF16, name="woven_lo", align_bytes=64, offset=AT_WOVEN_LO)
+        hi_parts = [quantise("hi0", woven_hi0, codes_hi0)]
+        woven_lo = keep.tile([P, PASSES * PART], BF16, name="woven_lo", align_bytes=64)
         weave_lo(woven_lo[:, 0:PART], lo_rows0[:])
         nc.gpsimd.tensor_tensor(
             woven_lo[:, PART : 2 * PART].rearrange("p (n i) -> p n i", i=PACK),
@@ -162,15 +159,18 @@ def tile_list_hwayt_hl_relu_kernel(
         minus_bias = keep.tile([P, N_TILES], F32, name="minus_bias", align_bytes=64, tag="lo_rows0")
         nc.scalar.activation(minus_bias[:], bias[:], ACT.Copy, scale=-1.0)
 
-        picked_words = shared.tile([P, J], U32, name="picked_words", align_bytes=64, offset=AT_PICKED)
+        picked = []
         for jt in range(J_TILES):
-            nc.vector.tensor_copy(picked_words[:, columns(jt)], words[:].indirect(entries(jt * J_TILE, (jt + 1) * J_TILE)))
+            tile = shared.tile([P, J_TILE], U32, name="picked%d" % jt, align_bytes=64, offset=AT_PICKED + 2 * KB * jt)
+            nc.vector.tensor_copy(tile[:], words[:].indirect(entries(jt * J_TILE, (jt + 1) * J_TILE)))
+            picked.append(tile)
         tab_codes = [keep.tile([P, PASSES, J_TILE], U16, name="tab_codes%d" % jt, align_bytes=64) for jt in range(J_TILES)]
-        for lo, hi in ((0, QUARTER), (QUARTER, J_TILE), (J_TILE, J)):
+        for jt, lo, hi in ((0, 0, QUARTER), (0, QUARTER, J_TILE), (1, 0, J_TILE)):
             nc.vector.tensor_copy(
-                tab_codes[lo // J_TILE][:, :, lo % J_TILE : lo % J_TILE + hi - lo],
-                picked_words[:, lo:hi].bitcast(U16).rearrange("p (j a) -> p a j", a=PASSES),
+                tab_codes[jt][:, :, lo:hi], picked[jt][:, lo:hi].bitcast(U16).rearrange("p (j a) -> p a j", a=PASSES)
             )
+        codes_hi1 = shared.tile([P, N], U32, name="codes_hi1", align_bytes=64, offset=AT_PICKED)
+        hi_parts.append(quantise("hi1", woven_hi1, codes_hi1))
         codes_lo = keep.tile([P, PASSES * N], U32, name="codes_lo", align_bytes=64)
         plane_lo = quantise("lo", woven_lo, codes_lo)[1]
 

@@ -37,7 +37,6 @@ AT_R1 = 0
 AT_WINDOW = 8 * KB - 256
 AT_RAW0 = 50 * KB
 AT_R0 = 10 * KB - 512
-AT_UPPER1 = 29 * KB
 AT_PICKED = 27 * KB + 512
 AT_MADE = 35 * KB
 AT_RESULT = 43 * KB
@@ -121,7 +120,7 @@ def tile_list_hwayt_hl_relu_kernel(
             nc.vector.quantize_mx(out=codes[:].bitcast(FP8X4), scales=plane[:], in_=woven[:])
             return codes, plane
 
-        hi_rows0 = keep.tile([P, PACK, N], F32, name="hi_rows0", align_bytes=64)
+        hi_rows0 = shared.tile([P, PACK, N], F32, name="hi_rows0", align_bytes=64, offset=AT_PICKED)
         for half in halves:
             nc.vector.tensor_scalar(
                 hi_rows0[:, half, :].bitcast(I32), wh_raw0[:, half, :].bitcast(I32), WORD_MASK, None, ALU.bitwise_and
@@ -142,9 +141,9 @@ def tile_list_hwayt_hl_relu_kernel(
         nc.sync.dma_start(out=r_rows1[:], in_=rT[P : 2 * P, :])
         r_rows = [r_rows0, r_rows1]
 
-        upper1 = shared.tile([P, PART], BF16, name="upper1", align_bytes=64, offset=AT_UPPER1)
+        upper1 = keep.tile([P, PART], BF16, name="upper1", align_bytes=64)
         weave_hi(upper1[:], wh_raw1[:].bitcast(BF16).rearrange("p i (n e) -> p i n e", e=2)[:, :, :, 1])
-        woven_hi1 = shared.tile([P, PART], BF16, name="woven_hi1", align_bytes=64, offset=AT_RAW0 + KB)
+        woven_hi1 = keep.tile([P, PART], BF16, name="woven_hi1", align_bytes=64)
         nc.vector.tensor_scalar(woven_hi1[:].bitcast(I32), upper1[:].bitcast(I32), PAIR_MASK, None, ALU.bitwise_and)
         codes_hi0 = shared.tile([P, N], U32, name="codes_hi0", align_bytes=64, offset=AT_RAW0)
         hi_parts = [quantise("hi0", woven_hi0, codes_hi0)]

@@ -22,7 +22,7 @@ PASSES = K // (P * PACK)
 N_TILES = N // P
 J_TILE = 512
 J_TILES = J // J_TILE
-QUARTER = J // 4
+HALF = J_TILE // 2
 QUAD = 32
 QUADS = P // QUAD
 ROWS = 4
@@ -35,15 +35,19 @@ PART = N * PACK
 KB = 1024
 AT_R1 = 0
 AT_WINDOW = 8 * KB - 256
-AT_RAW0 = 50 * KB
 AT_R0 = 10 * KB - 512
 AT_PICKED = 27 * KB + 512
 AT_MADE = 35 * KB
 AT_RESULT = 43 * KB
+AT_RAW0 = 50 * KB
 
 
 def columns(jt):
     return slice(jt * J_TILE, (jt + 1) * J_TILE)
+
+
+def own(c):
+    return slice(c * P, (c + 1) * P)
 
 
 def tile_list_hwayt_hl_relu_kernel(
@@ -63,9 +67,9 @@ def tile_list_hwayt_hl_relu_kernel(
             for piece in pieces:
                 nc.sync.dma_start(out=raw[:, piece, :], in_=rows[:, piece, :])
 
-        halves = [slice(0, PACK // 2), slice(PACK // 2, PACK)]
+        row_pairs = [slice(0, PACK // 2), slice(PACK // 2, PACK)]
         wh_raw0 = shared.tile([P, PACK, N], F32, name="wh_raw0", align_bytes=64, offset=AT_RAW0)
-        load_wh(0, wh_raw0, halves)
+        load_wh(0, wh_raw0, row_pairs)
         offsets = keep.tile([P, J // 16], U16, name="offsets")
         nc.sync.dma_start(offsets[:], offs)
 
@@ -102,33 +106,29 @@ def tile_list_hwayt_hl_relu_kernel(
         nc.gpsimd.memset(zeros[:], 0.0)
         nc.scalar.activation(warm[:], zeros[:], ACT.Sigmoid)
 
-        def own(c):
-            return slice(c * P, (c + 1) * P)
-
-        def weave_hi(woven, rows):
+        def weave_by_fours(woven, rows):
             nc.scalar.copy(
                 out=woven.rearrange("p (g m i) -> p g i m", m=PACK, i=PACK),
                 in_=rows.rearrange("p i (g m) -> p g i m", m=PACK),
             )
 
-        def weave_lo(woven, rows):
+        def weave(woven, rows):
             nc.scalar.copy(out=woven.rearrange("p (n i) -> p n i", i=PACK), in_=rows.rearrange("p i n -> p n i"))
 
         def quantise(name, woven, codes):
-            width = codes.shape[1]
-            plane = keep.tile([P, width], U8, name="plane" + name, align_bytes=64)
+            plane = keep.tile([P, codes.shape[1]], U8, name="plane_" + name, align_bytes=64)
             nc.vector.quantize_mx(out=codes[:].bitcast(FP8X4), scales=plane[:], in_=woven[:])
             return codes, plane
 
         hi_rows0 = shared.tile([P, PACK, N], F32, name="hi_rows0", align_bytes=64, offset=AT_PICKED)
-        for half in halves:
+        for pair in row_pairs:
             nc.vector.tensor_scalar(
-                hi_rows0[:, half, :].bitcast(I32), wh_raw0[:, half, :].bitcast(I32), WORD_MASK, None, ALU.bitwise_and
+                hi_rows0[:, pair, :].bitcast(I32), wh_raw0[:, pair, :].bitcast(I32), WORD_MASK, None, ALU.bitwise_and
             )
         lo_rows0 = keep.tile([P, PACK, N], BF16, name="lo_rows0", align_bytes=64, tag="lo_rows0")
         nc.gpsimd.tensor_tensor(lo_rows0[:], wh_raw0[:], hi_rows0[:], ALU.subtract)
         woven_hi0 = keep.tile([P, PART], BF16, name="woven_hi0", align_bytes=64)
-        weave_hi(woven_hi0[:], hi_rows0[:])
+        weave_by_fours(woven_hi0[:], hi_rows0[:])
 
         picked_scales = keep.tile([P, J], U8, name="picked_scales", align_bytes=64)
         nc.vector.tensor_copy(picked_scales[:], scale_rows[:].indirect(offsets[:]))
@@ -141,37 +141,39 @@ def tile_list_hwayt_hl_relu_kernel(
         nc.sync.dma_start(out=r_rows1[:], in_=rT[P : 2 * P, :])
         r_rows = [r_rows0, r_rows1]
 
-        upper1 = keep.tile([P, PART], BF16, name="upper1", align_bytes=64)
-        weave_hi(upper1[:], wh_raw1[:].bitcast(BF16).rearrange("p i (n e) -> p i n e", e=2)[:, :, :, 1])
-        woven_hi1 = keep.tile([P, PART], BF16, name="woven_hi1", align_bytes=64)
-        nc.vector.tensor_scalar(woven_hi1[:].bitcast(I32), upper1[:].bitcast(I32), PAIR_MASK, None, ALU.bitwise_and)
+        upper1 = keep.tile([P, PACK, N], BF16, name="upper1", align_bytes=64)
+        nc.scalar.copy(out=upper1[:], in_=wh_raw1[:].bitcast(BF16).rearrange("p i (n e) -> p i n e", e=2)[:, :, :, 1])
+        hi_rows1 = keep.tile([P, PACK, N], BF16, name="hi_rows1", align_bytes=64)
+        nc.vector.tensor_scalar(hi_rows1[:].bitcast(I32), upper1[:].bitcast(I32), PAIR_MASK, None, ALU.bitwise_and)
         codes_hi0 = shared.tile([P, N], U32, name="codes_hi0", align_bytes=64, offset=AT_RAW0)
         hi_parts = [quantise("hi0", woven_hi0, codes_hi0)]
         woven_lo = keep.tile([P, PASSES * PART], BF16, name="woven_lo", align_bytes=64)
-        weave_lo(woven_lo[:, 0:PART], lo_rows0[:])
-        nc.gpsimd.tensor_tensor(
-            woven_lo[:, PART : 2 * PART].rearrange("p (n i) -> p n i", i=PACK),
-            wh_raw1[:].rearrange("p i n -> p n i"),
-            woven_hi1[:].rearrange("p (n i) -> p n i", i=PACK),
-            ALU.subtract,
-        )
+        weave(woven_lo[:, 0:PART], lo_rows0[:])
+        lo_rows1 = keep.tile([P, PACK, N], BF16, name="lo_rows1", align_bytes=64)
+        nc.gpsimd.tensor_tensor(lo_rows1[:], wh_raw1[:], hi_rows1[:], ALU.subtract)
+        woven_hi1 = keep.tile([P, PART], BF16, name="woven_hi1", align_bytes=64)
+        weave(woven_hi1[:], hi_rows1[:])
         minus_bias = keep.tile([P, N_TILES], F32, name="minus_bias", align_bytes=64, tag="lo_rows0")
         nc.scalar.activation(minus_bias[:], bias[:], ACT.Copy, scale=-1.0)
+
+        weave(woven_lo[:, PART : 2 * PART], lo_rows1[:])
 
         picked = []
         for jt in range(J_TILES):
             tile = shared.tile([P, J_TILE], U32, name="picked%d" % jt, align_bytes=64, offset=AT_PICKED + 2 * KB * jt)
             nc.vector.tensor_copy(tile[:], words[:].indirect(entries(jt * J_TILE, (jt + 1) * J_TILE)))
             picked.append(tile)
-        tab_codes = [keep.tile([P, PASSES, J_TILE], U16, name="tab_codes%d" % jt, align_bytes=64) for jt in range(J_TILES)]
-        for jt, lo, hi in ((0, 0, QUARTER), (0, QUARTER, J_TILE), (1, 0, J_TILE)):
+        tab_codes = [
+            keep.tile([P, PASSES, J_TILE], U16, name="tab_codes%d" % jt, align_bytes=64) for jt in range(J_TILES)
+        ]
+        for jt, lo, hi in ((0, 0, HALF), (0, HALF, J_TILE), (1, 0, J_TILE)):
             nc.vector.tensor_copy(
                 tab_codes[jt][:, :, lo:hi], picked[jt][:, lo:hi].bitcast(U16).rearrange("p (j a) -> p a j", a=PASSES)
             )
         codes_hi1 = shared.tile([P, N], U32, name="codes_hi1", align_bytes=64, offset=AT_PICKED)
         hi_parts.append(quantise("hi1", woven_hi1, codes_hi1))
         codes_lo = keep.tile([P, PASSES * N], U32, name="codes_lo", align_bytes=64)
-        plane_lo = quantise("lo", woven_lo, codes_lo)[1]
+        codes_lo, plane_lo = quantise("lo", woven_lo, codes_lo)
 
         def multiply(acc, weights, weight_plane, a, jt, cols, start, stop):
             nc.tensor.matmul_mx(
@@ -184,42 +186,34 @@ def tile_list_hwayt_hl_relu_kernel(
                 stop=stop,
             )
 
-        whole, left, right = slice(0, J_TILE), slice(0, QUARTER), slice(QUARTER, J_TILE)
+        whole, left, right = slice(0, J_TILE), slice(0, HALF), slice(HALF, J_TILE)
         blocks = [(c, jt) for c in range(N_TILES) for jt in range(J_TILES)]
-        ha, carry = {}, {}
+        pieces = {(c, jt): (left, right) if c == 0 else (whole,) for c, jt in blocks}
+        carry = {}
         for c, jt in blocks:
             if (c, jt) == (1, 0):
                 carry[c, jt] = shared.tile([P, J_TILE], F32, name="carry10", align_bytes=64, offset=AT_MADE)
             else:
                 carry[c, jt] = keep.tile([P, J_TILE], F32, name="carry%d%d" % (c, jt), align_bytes=64)
 
-        def gate_passes(acc, c, jt, cols):
+        for bank, (c, jt, cols) in enumerate([(c, jt, cols) for c, jt in blocks for cols in pieces[c, jt]]):
+            ga = psum.tile([P, J_TILE], F32, name="ga%d" % bank, tag="bank%d" % bank)
             for a in reversed(range(PASSES)):
                 weights = wg_codes[:, a, 2 * c * P : 2 * (c + 1) * P].bitcast(FP4X4)
-                multiply(acc, weights, wg_planes[:, a, own(c)], a, jt, cols, a == PASSES - 1, a == 0)
-
-        def sigmoid(acc, c, jt, cols):
+                multiply(ga, weights, wg_planes[:, a, own(c)], a, jt, cols, a == PASSES - 1, a == 0)
             nc.scalar.activation(
-                carry[c, jt][:, cols], acc[:, cols], ACT.Sigmoid, bias=minus_bias[:, c : c + 1], scale=-1.0
+                carry[c, jt][:, cols], ga[:, cols], ACT.Sigmoid, bias=minus_bias[:, c : c + 1], scale=-1.0
             )
 
-        def bank(name, tag):
-            return psum.tile([P, J_TILE], F32, name=name, tag=tag)
-
-        for (c, jt, cols), tag in zip(
-            ((0, 0, left), (0, 0, right), (0, 1, left), (0, 1, right), (1, 0, whole), (1, 1, whole)), range(6)
-        ):
-            acc = bank("ga%d" % tag, "bank%d" % tag)
-            gate_passes(acc, c, jt, cols)
-            sigmoid(acc, c, jt, cols)
-        for (c, jt), tag in zip(blocks, range(4)):
-            ha[c, jt] = bank("ha%d%d" % (c, jt), "bank%d" % tag)
-            for a in range(PASSES):
-                codes, plane = hi_parts[a]
+        ha = {}
+        for bank, (c, jt) in enumerate(blocks):
+            ha[c, jt] = psum.tile([P, J_TILE], F32, name="ha%d%d" % (c, jt), tag="bank%d" % bank)
+            for a, (codes, plane) in enumerate(hi_parts):
                 multiply(ha[c, jt], codes[:, own(c)].bitcast(FP8X4), plane[:, own(c)], a, jt, whole, a == 0, False)
             for a in range(PASSES):
-                cols = slice(a * N + c * P, a * N + (c + 1) * P)
-                multiply(ha[c, jt], codes_lo[:, cols].bitcast(FP8X4), plane_lo[:, cols], a, jt, whole, False, a == PASSES - 1)
+                lo_cols = slice(a * N + c * P, a * N + (c + 1) * P)
+                weights = codes_lo[:, lo_cols].bitcast(FP8X4)
+                multiply(ha[c, jt], weights, plane_lo[:, lo_cols], a, jt, whole, False, a == PASSES - 1)
 
         kept = {}
         for c, jt in blocks:
@@ -227,7 +221,7 @@ def tile_list_hwayt_hl_relu_kernel(
                 kept[c, jt] = shared.tile([P, J_TILE], F32, name="kept00", align_bytes=64, offset=AT_RESULT)
             else:
                 kept[c, jt] = keep.tile([P, J_TILE], F32, name="kept%d%d" % (c, jt), align_bytes=64)
-            for cols in (left, right) if c == 0 else (whole,):
+            for cols in pieces[c, jt]:
                 window = r_rows[c][:].indirect(entries(jt * J_TILE + cols.start, jt * J_TILE + cols.stop))
                 nc.vector.tensor_tensor(kept[c, jt][:, cols], window, carry[c, jt][:, cols], ALU.mult)
 
@@ -247,7 +241,7 @@ def tile_list_hwayt_hl_relu_kernel(
 
         first = keep.tile([P, J_TILE], F32, name="first", align_bytes=64)
         add_and_store(nc.gpsimd, first[:], 0, 0, (0, J_TILE))
-        result = shared.tile([P, 3, J_TILE], F32, name="result", align_bytes=64, offset=AT_RESULT)
+        result = shared.tile([P, len(blocks) - 1, J_TILE], F32, name="result", align_bytes=64, offset=AT_RESULT)
         add_and_store(nc.vector, result[:, 0, :], 0, 1, (0, STORE, J_TILE))
         add_and_store(nc.vector, result[:, 1, :], 1, 0, (0, STORE, J_TILE))
         add_and_store(nc.vector, result[:, 2, :], 1, 1, (0, STORE, J_TILE - STORE // 2, J_TILE))

from contextlib import ExitStack

import concourse.mybir as mybir

K, N, T, J = 1024, 256, 2048, 1024
FLOPS = 3 * 2 * K * N * J

F32 = mybir.dt.float32
BF16 = mybir.dt.bfloat16
I32 = mybir.dt.int32
U32 = mybir.dt.uint32
U16 = mybir.dt.uint16
U8 = mybir.dt.uint8
FP8X4 = mybir.dt.float8_e4m3fn_x4
FP4X4 = mybir.dt.float4_e2m1fn_x4
ALU = mybir.AluOpType
ACT = mybir.ActivationFunctionType

P = 128
PACK = 4
PASSES = K // (P * PACK)
N_TILES = N // P
J_TILE = 512
J_TILES = J // J_TILE
HALF = J_TILE // 2
QUAD = 32
QUADS = P // QUAD
ROWS = 4
STORE = 256
SHIFT = 16
WORD_MASK = 0xFFF00000 - (1 << 32)
PAIR_MASK = 0xFFF0FFF0 - (1 << 32)
PART = N * PACK

KB = 1024
AT_R1 = 0
AT_WINDOW = 8 * KB - 256
AT_R0 = 10 * KB - 512
AT_PICKED = 27 * KB + 512
AT_MADE = 35 * KB
AT_RESULT = 43 * KB
AT_RAW0 = 50 * KB


def columns(jt):
    return slice(jt * J_TILE, (jt + 1) * J_TILE)


def own(c):
    return slice(c * P, (c + 1) * P)


def tile_list_hwayt_hl_relu_kernel(
    tc, tab_words, tab_scales, wg_words, wg_scales, wh, bg, rT, offs, out
):
    nc = tc.nc
    with ExitStack() as ctx:
        keep = ctx.enter_context(tc.tile_pool(name="keep", bufs=1))
        shared = ctx.enter_context(tc.tile_pool(name="shared", bufs=1))
        psum = ctx.enter_context(tc.psum_pool(name="psum", bufs=1))

        def entries(lo, hi):
            return offsets[:, lo // 16 : hi // 16]

        def load_wh(a, raw, pieces):
            rows = wh[a * P * PACK : (a + 1) * P * PACK, :].rearrange("(p i) n -> p i n", i=PACK)
            for piece in pieces:
                nc.sync.dma_start(out=raw[:, piece, :], in_=rows[:, piece, :])

        row_pairs = [slice(0, PACK // 2), slice(PACK // 2, PACK)]
        wh_raw0 = shared.tile([P, PACK, N], F32, name="wh_raw0", align_bytes=64, offset=AT_RAW0)
        load_wh(0, wh_raw0, row_pairs)
        offsets = keep.tile([P, J // 16], U16, name="offsets")
        nc.sync.dma_start(offsets[:], offs)

        scale_rows = shared.tile([P, T], U8, name="scale_rows", align_bytes=64, offset=AT_WINDOW)
        nc.gpsimd.memset(scale_rows[:].bitcast(I32), 0)
        for r in range(ROWS):
            nc.sync.dma_start(
                out=scale_rows[r:P:SHIFT, :].bitcast(I32),
                in_=tab_scales[:, r : QUADS * ROWS : ROWS, :].rearrange("a q t -> q a t").bitcast(I32),
            )
        wh_raw1 = keep.tile([P, PACK, N], F32, name="wh_raw1", align_bytes=64)
        load_wh(1, wh_raw1, [slice(0, PACK)])
        words = keep.tile([P, T], U32, name="words", align_bytes=64)
        nc.sync.dma_start(out=words[:].bitcast(I32), in_=tab_words[0].rearrange("p t b -> p (t b)").bitcast(I32))

        wg_codes = keep.tile([P, PASSES, 2 * N], U8, name="wg_codes", align_bytes=64)
        nc.sync.dma_start(out=wg_codes[:].bitcast(I32), in_=wg_words.rearrange("a p b -> p a b").bitcast(I32))
        wg_planes = keep.tile([P, PASSES, N], U8, name="wg_planes", align_bytes=64)
        nc.gpsimd.memset(wg_planes[:].bitcast(I32), 0)
        for q in range(QUADS):
            nc.sync.dma_start(
                out=wg_planes[QUAD * q : QUAD * q + ROWS, :, :].bitcast(I32),
                in_=wg_scales[:, ROWS * q : ROWS * (q + 1), :].rearrange("a r n -> r a n").bitcast(I32),
            )
        bias = keep.tile([P, N_TILES], F32, name="bias")
        with nc.allow_non_contiguous_dma(reason="one bias value for each partition"):
            nc.sync.dma_start(out=bias[:], in_=bg.rearrange("(c p) -> p c", p=P))

        tab_plane1 = keep.tile([P, J], U8, name="tab_plane1", align_bytes=64)
        nc.vector.memset(tab_plane1[P - QUAD : P, :].bitcast(I32), 0)

        warm = keep.tile([P, N_TILES], F32, name="warm")
        zeros = keep.tile([P, N_TILES], F32, name="zeros")
        nc.gpsimd.memset(zeros[:], 0.0)
        nc.scalar.activation(warm[:], zeros[:], ACT.Sigmoid)

        def weave_by_fours(woven, rows):
            nc.scalar.copy(
                out=woven.rearrange("p (g m i) -> p g i m", m=PACK, i=PACK),
                in_=rows.rearrange("p i (g m) -> p g i m", m=PACK),
            )

        def weave(woven, rows):
            nc.scalar.copy(out=woven.rearrange("p (n i) -> p n i", i=PACK), in_=rows.rearrange("p i n -> p n i"))

        def quantise(name, woven, codes):
            plane = keep.tile([P, codes.shape[1]], U8, name="plane_" + name, align_bytes=64)
            nc.vector.quantize_mx(out=codes[:].bitcast(FP8X4), scales=plane[:], in_=woven[:])
            return codes, plane

        hi_rows0 = shared.tile([P, PACK, N], F32, name="hi_rows0", align_bytes=64, offset=AT_PICKED)
        for pair in row_pairs:
            nc.vector.tensor_scalar(
                hi_rows0[:, pair, :].bitcast(I32), wh_raw0[:, pair, :].bitcast(I32), WORD_MASK, None, ALU.bitwise_and
            )
        lo_rows0 = keep.tile([P, PACK, N], BF16, name="lo_rows0", align_bytes=64, tag="lo_rows0")
        nc.gpsimd.tensor_tensor(lo_rows0[:], wh_raw0[:], hi_rows0[:], ALU.subtract)
        woven_hi0 = keep.tile([P, PART], BF16, name="woven_hi0", align_bytes=64)
        weave_by_fours(woven_hi0[:], hi_rows0[:])

        picked_scales = keep.tile([P, J], U8, name="picked_scales", align_bytes=64)
        nc.vector.tensor_copy(picked_scales[:], scale_rows[:].indirect(offsets[:]))
        nc.sync.dma_start(out=tab_plane1[0 : P - SHIFT, :].bitcast(I32), in_=picked_scales[SHIFT:P, :].bitcast(I32))
        tab_planes = [picked_scales, tab_plane1]

        r_rows0 = shared.tile([P, T], F32, name="r_rows0", align_bytes=64, offset=AT_R0)
        nc.sync.dma_start(out=r_rows0[:], in_=rT[0:P, :])
        r_rows1 = shared.tile([P, T], F32, name="r_rows1", align_bytes=64, offset=AT_R1)
        nc.sync.dma_start(out=r_rows1[:], in_=rT[P : 2 * P, :])
        r_rows = [r_rows0, r_rows1]

        upper1 = keep.tile([P, PACK, N], BF16, name="upper1", align_bytes=64)
        nc.scalar.copy(out=upper1[:], in_=wh_raw1[:].bitcast(BF16).rearrange("p i (n e) -> p i n e", e=2)[:, :, :, 1])
        hi_rows1 = keep.tile([P, PACK, N], BF16, name="hi_rows1", align_bytes=64)
        nc.vector.tensor_scalar(hi_rows1[:].bitcast(I32), upper1[:].bitcast(I32), PAIR_MASK, None, ALU.bitwise_and)
        codes_hi0 = shared.tile([P, N], U32, name="codes_hi0", align_bytes=64, offset=AT_RAW0)
        hi_parts = [quantise("hi0", woven_hi0, codes_hi0)]
        woven_lo = keep.tile([P, PASSES * PART], BF16, name="woven_lo", align_bytes=64)
        weave(woven_lo[:, 0:PART], lo_rows0[:])
        lo_rows1 = keep.tile([P, PACK, N], BF16, name="lo_rows1", align_bytes=64)
        nc.gpsimd.tensor_tensor(lo_rows1[:], wh_raw1[:], hi_rows1[:], ALU.subtract)
        woven_hi1 = keep.tile([P, PART], BF16, name="woven_hi1", align_bytes=64)
        weave(woven_hi1[:], hi_rows1[:])
        minus_bias = keep.tile([P, N_TILES], F32, name="minus_bias", align_bytes=64, tag="lo_rows0")
        nc.scalar.activation(minus_bias[:], bias[:], ACT.Copy, scale=-1.0)

        weave(woven_lo[:, PART : 2 * PART], lo_rows1[:])

        picked = []
        for jt in range(J_TILES):
            tile = shared.tile([P, J_TILE], U32, name="picked%d" % jt, align_bytes=64, offset=AT_PICKED + 2 * KB * jt)
            nc.vector.tensor_copy(tile[:], words[:].indirect(entries(jt * J_TILE, (jt + 1) * J_TILE)))
            picked.append(tile)
        tab_codes = [
            keep.tile([P, PASSES, J_TILE], U16, name="tab_codes%d" % jt, align_bytes=64) for jt in range(J_TILES)
        ]
        for jt, lo, hi in ((0, 0, HALF), (0, HALF, J_TILE), (1, 0, J_TILE)):
            nc.vector.tensor_copy(
                tab_codes[jt][:, :, lo:hi], picked[jt][:, lo:hi].bitcast(U16).rearrange("p (j a) -> p a j", a=PASSES)
            )
        codes_hi1 = shared.tile([P, N], U32, name="codes_hi1", align_bytes=64, offset=AT_PICKED)
        hi_parts.append(quantise("hi1", woven_hi1, codes_hi1))
        codes_lo = keep.tile([P, PASSES * N], U32, name="codes_lo", align_bytes=64)
        codes_lo, plane_lo = quantise("lo", woven_lo, codes_lo)

        def multiply(acc, weights, weight_plane, a, jt, cols, start, stop):
            nc.tensor.matmul_mx(
                out=acc[:, cols],
                lhsT=weights,
                lhsT_scale=weight_plane,
                rhs=tab_codes[jt][:, a, cols].bitcast(U8).bitcast(FP4X4),
                rhs_scale=tab_planes[a][:, columns(jt)][:, cols],
                start=start,
                stop=stop,
            )

        whole, left, right = slice(0, J_TILE), slice(0, HALF), slice(HALF, J_TILE)
        blocks = [(c, jt) for c in range(N_TILES) for jt in range(J_TILES)]
        pieces = {(c, jt): (left, right) if c == 0 else (whole,) for c, jt in blocks}
        carry = {}
        for c, jt in blocks:
            if (c, jt) == (1, 0):
                carry[c, jt] = shared.tile([P, J_TILE], F32, name="carry10", align_bytes=64, offset=AT_MADE)
            else:
                carry[c, jt] = keep.tile([P, J_TILE], F32, name="carry%d%d" % (c, jt), align_bytes=64)

        for bank, (c, jt, cols) in enumerate([(c, jt, cols) for c, jt in blocks for cols in pieces[c, jt]]):
            ga = psum.tile([P, J_TILE], F32, name="ga%d" % bank, tag="bank%d" % bank)
            for a in reversed(range(PASSES)):
                weights = wg_codes[:, a, 2 * c * P : 2 * (c + 1) * P].bitcast(FP4X4)
                multiply(ga, weights, wg_planes[:, a, own(c)], a, jt, cols, a == PASSES - 1, a == 0)
            nc.scalar.activation(
                carry[c, jt][:, cols], ga[:, cols], ACT.Sigmoid, bias=minus_bias[:, c : c + 1], scale=-1.0
            )

        ha = {}
        for bank, (c, jt) in enumerate(blocks):
            ha[c, jt] = psum.tile([P, J_TILE], F32, name="ha%d%d" % (c, jt), tag="bank%d" % bank)
            for a, (codes, plane) in enumerate(hi_parts):
                multiply(ha[c, jt], codes[:, own(c)].bitcast(FP8X4), plane[:, own(c)], a, jt, whole, a == 0, False)
            for a in range(PASSES):
                lo_cols = slice(a * N + c * P, a * N + (c + 1) * P)
                weights = codes_lo[:, lo_cols].bitcast(FP8X4)
                multiply(ha[c, jt], weights, plane_lo[:, lo_cols], a, jt, whole, False, a == PASSES - 1)

        kept = {}
        for c, jt in blocks:
            if (c, jt) == (0, 0):
                kept[c, jt] = shared.tile([P, J_TILE], F32, name="kept00", align_bytes=64, offset=AT_RESULT)
            else:
                kept[c, jt] = keep.tile([P, J_TILE], F32, name="kept%d%d" % (c, jt), align_bytes=64)
            for cols in pieces[c, jt]:
                window = r_rows[c][:].indirect(entries(jt * J_TILE + cols.start, jt * J_TILE + cols.stop))
                nc.vector.tensor_tensor(kept[c, jt][:, cols], window, carry[c, jt][:, cols], ALU.mult)

        gates = shared.tile([P, N_TILES, J], F32, name="gates", align_bytes=64, offset=AT_R0)
        made = shared.tile([P, N_TILES, J], F32, name="made", align_bytes=64, offset=AT_MADE)
        for c, jt in blocks:
            nc.scalar.activation(gates[:, c, columns(jt)], carry[c, jt][:], ACT.Copy, bias=1.0, scale=-1.0)
            nc.vector.scalar_tensor_tensor(
                made[:, c, columns(jt)], ha[c, jt][:], 0.0, gates[:, c, columns(jt)], ALU.max, ALU.mult
            )

        def add_and_store(engine, result, c, jt, edges):
            for lo, hi in zip(edges, edges[1:]):
                span = slice(jt * J_TILE + lo, jt * J_TILE + hi)
                engine.tensor_tensor(result[:, lo:hi], made[:, c, span], kept[c, jt][:, lo:hi], ALU.add)
                nc.sync.dma_start(out=out[own(c), span], in_=result[:, lo:hi])

        first = keep.tile([P, J_TILE], F32, name="first", align_bytes=64)
        add_and_store(nc.gpsimd, first[:], 0, 0, (0, J_TILE))
        result = shared.tile([P, len(blocks) - 1, J_TILE], F32, name="result", align_bytes=64, offset=AT_RESULT)
        add_and_store(nc.vector, result[:, 0, :], 0, 1, (0, STORE, J_TILE))
        add_and_store(nc.vector, result[:, 1, :], 1, 0, (0, STORE, J_TILE))
        add_and_store(nc.vector, result[:, 2, :], 1, 1, (0, STORE, J_TILE - STORE // 2, J_TILE))
